import numpy as np, ml_dtypes
CORES = [24,25,26,27,28,29,30,31]
N = 8
BF = ml_dtypes.bfloat16
P, V, C, PH, S, Z, CAP, RO = 2048, 1024, 1024, 2, 4, 4, 128, 3
I = V // PH
def tail(rng, b, top):
    return np.where(np.arange(16)[:, None] >= rng.integers(0, 17, (N, 8, 1, V)), rng.integers(0, top, b.shape), b)
def parts(rng):
    e = rng.choice(np.array([10.0, 14.0, 18.0, 24.0]), (N, 8, 1, 1))
    x = np.minimum((256 * rng.random((N, 8, 16, P)) ** e).astype(np.int64), 255)
    m = rng.integers(0, 256, (N, 8, 16, V)); b = rng.integers(0, P, (N, 8, 16, V))
    return x, m, b, tail(rng, b, P), rng.integers(0, V, (N, 8, 16, C))
def tops(x, l):
    y = np.take_along_axis(x, l[:, :, 0][:, :, None, :], 3)
    for k in range(1, 16): y = np.maximum(y, np.take_along_axis(x, l[:, :, k][:, :, None, :], 3))
    return y
def late(rng, shape):
    return PH * rng.integers(0, I, shape) + 1 + rng.integers(0, PH - 1, shape)
def pack(x, m, b, d, u):
    r = {"mor": x.reshape(N, 128, P).astype(np.float32).astype(BF), "mea": m.reshape(N, 128, V).astype(np.float32).astype(BF)}
    r["bas"] = b.reshape(N, 128, V).astype(np.int32); r["der"] = d.reshape(N, 128, V).astype(np.int32); r["use"] = u.reshape(N, 128, C).astype(np.int32)
    return r
def setup_inputs(rng):
    x, m, b, d, u = parts(rng); h = rng.integers(0, 8, N)
    for q in range(N):
        g = int(h[q]); x[q, g, :, P - 1] = 255; m[q, g] = rng.integers(0, 151, (16, V)); u[q, g] = late(rng, (16, C))
        d[q, g, rng.integers(0, 16, I), PH * np.arange(I)] = P - 1
    near = rng.random((N, 8, 1, V)) < rng.choice(np.array([0.0, 0.2, 0.5, 0.8]), (N, 8, 1, 1)); near[np.arange(N), h] = False
    m = np.where(near, np.clip(tops(x, d) + rng.integers(-24, 25, m.shape), 0, 255), m)
    for q in range(N):
        for g in range(8):
            v = PH * rng.permutation(I)[:3]; u[q, g][:, b[q, g, 15, v] & (C - 1)] = v
    return pack(x, m, b, d, u)
def setup_inputs_corners(rng):
    x, m, b, d, u = parts(rng); x = np.minimum(x, 100); x[..., P - 1] = 255; m = rng.integers(0, 101, m.shape)
    b = rng.integers(0, P - 1, b.shape); d = tail(rng, b, P - 1); u = late(rng, u.shape)
    u = np.where(rng.random((N, 8, 1, C)) < 0.1, np.where(rng.random((N, 8, 1, C)) < 0.5, V - 1, 1), u); top = tops(x, d)
    for q in range(N):
        for g in range(8):
            if q == 3 and g % 2 == 1:
                n = (0, 1, CAP // 2, CAP - 1)[g // 2]; o = PH * np.arange(I); w = PH * rng.permutation(I) + 1
                m[q, g][:, o] = top[q, g][:, o]; m[q, g][:, w[:n]] = top[q, g][:, w[:n]]
                d[q, g, rng.integers(0, 16, I - n), w[n:]] = P - 1; u[q, g] = PH * rng.integers(0, I, (16, C))
                continue
            n = int(rng.choice(np.array([0, 1, CAP - 1, CAP, CAP + 1, I])))
            if q == 0: n = (CAP, CAP + 1, I, CAP - 1, 1, 0, CAP, CAP + 1)[g]
            if q == 1 or q == 2: n = (CAP, 1, CAP - 1, 0)[g % 4]
            if q == 2 and g == 7: n = CAP + 1
            o = PH * rng.permutation(I); nl = min(n, C // 2); lone, fit, ad = o[:nl], o[nl:n], o[n:]
            cols = 2 * rng.permutation(C // 2)[:nl] + q % 2
            b[q, g, 15, lone] = cols + C * rng.integers(0, P // C - 1, nl); u[q, g][:, cols] = lone
            b[q, g, 15, ad] = 2 * rng.integers(0, C // 2, I - n) + 1 - q % 2 + C * rng.integers(0, P // C - 1, I - n)
            bad = np.concatenate([lone, ad]); d[q, g, rng.integers(0, 16, len(bad)), bad] = P - 1
            m[q, g][:, fit] = top[q, g][:, fit]
            if q == 2:
                o = PH * np.arange(I); z = np.add.reduce(np.arange(1, 17)[:, None] * m[q, g][:, o], axis=0) & (Z - 1)
                left = np.ones(P, dtype=bool); left[P - 1] = False; left[S * np.arange(I) + z] = False
                l = d[q, g][:, o + 1]; l = np.where(left[l], l, rng.choice(np.flatnonzero(left), l.shape))
                d[q, g][:, o + 1] = l; m[q, g][:, o + 1] = np.maximum.reduce(x[q, g][:, l], axis=1)
    return pack(x, m, b, d, u)
def setup_inputs_ties(rng):
    x, m, b, d, u = parts(rng); x[:, 1::2] = x[:, 1::2] >> 6
    k = rng.integers(0, 8, (N, 8, 1, V)); m = np.take_along_axis(m[..., :8], k, 3); m[:, 1::2] = m[:, 1::2] >> 6
    b[:, :2] = np.take_along_axis(b[:, :2, :, :8], k[:, :2], 3); d[:, :2] = np.take_along_axis(d[:, :2, :, :8], k[:, :2], 3)
    lane = np.arange(V); a = rng.integers(40, 81, (N, 16, 1)); high = (np.arange(16)[:, None] == 15) & (lane >= V // 2)
    m[:, 6] = np.where(lane % PH == 0, rng.integers(215, 256, (N, 16, V)), a + high); u[:, 6] = late(rng, (N, 16, C))
    u[..., ::2] = u[:, :, np.arange(16) & 3, ::2]
    return pack(x, m, b, d, u)
def setup_inputs_alike(rng):
    x, m, b, d, u = parts(rng)
    d[:, :3] = b[:, :3]; d[:, 1, 0] = (b[:, 1, 0] + 1) % P; d[:, 2, 15] = (b[:, 2, 15] + 1) % P
    b[:, 3, 15] = rng.integers(0, P, (N, 1)); u[:, 4] = rng.integers(0, V, (N, 1, C))
    for q in range(N):
        v = PH * rng.permutation(I)[:I // 4]; u[q, 4][:, b[q, 4, 15, v] & (C - 1)] = v
    b[:, 5] = rng.integers(0, P, (N, 1, V)); d[:, 5] = rng.integers(0, P, (N, 1, V)); u[:, 6] = (V - 1) * rng.integers(0, 2, (N, 16, C))
    for q in range(N):
        v = PH * rng.permutation(I)[:I // 8]; c = b[q, 7, 15, v] & (C - 1); u[q, 7][:, c] = v; u[(q + 1) % N, 7][:, c] = v
    return pack(x, m, b, d, u)
def setup_inputs_spread(rng):
    x = (np.exp2(8 * rng.random((N, 8, 1, P))) * rng.random((N, 8, 16, P)) ** 3).astype(np.int64)
    m = (np.exp2(8 * rng.random((N, 8, 1, V))) * rng.random((N, 8, 16, V))).astype(np.int64)
    e = rng.choice(np.array([1.0, 2.0, 4.0, 8.0]), (3, N, 8, 1, 1))
    b = (P * rng.random((N, 8, 16, V)) ** e[0]).astype(np.int64); c = (P * rng.random((N, 8, 16, V)) ** e[1]).astype(np.int64)
    d = np.where(np.arange(16)[:, None] >= rng.integers(0, 17, (N, 8, 1, V)), c, b); u = (V * rng.random((N, 8, 16, C)) ** e[2]).astype(np.int64)
    return pack(np.clip(x, 0, 255), np.clip(m, 0, 255), np.clip(b, 0, P - 1), np.clip(d, 0, P - 1), np.clip(u, 0, V - 1))
def setup_inputs_ends(rng):
    def bits(p, n): return 255 * (rng.random((N, 8, 16, n)) < p)
    def lists(n, hi):
        k = rng.random((N, 8, 1, n)); a = hi * rng.integers(0, 2, (N, 8, 16, n))
        return np.where(k < 0.25, 0, np.where(k < 0.5, hi, np.where(k < 0.8, a, rng.integers(0, hi + 1, (N, 8, 16, n)))))
    k = rng.random((N, 8, 1, P)); x = np.where(k < 0.6, 0, np.where(k < 0.63, 255, bits(0.06, P)))
    k = rng.random((N, 8, 1, V)); m = np.where(k < 0.25, 0, np.where(k < 0.5, 255, bits(0.5, V)))
    b = lists(V, P - 1); d = np.where(np.arange(16)[:, None] >= rng.integers(0, 17, (N, 8, 1, V)), lists(V, P - 1), b); u = lists(C, V - 1)
    for t in range(RO):
        for c in (97 * t, 97 * t - 1):
            u[..., c & (C - 1)] = np.where(rng.random((N, 8, 16)) < 0.5, (V - 1) * rng.integers(0, 2, (N, 8, 16)), rng.integers(0, V, (N, 8, 16)))
    x[:, ::2, :, 0] = 255 * rng.integers(0, 2, (N, 4, 16)); x[:, ::2, :, P - 1] = 255 * rng.integers(0, 2, (N, 4, 16)); x[:, 1::2, :, 0] = 0; x[:, 1::2, :, P - 1] = 255
    lo, hi = PH - 1 + PH * (PH % 2), V - 1 - PH
    m[:, 1::2, :, :PH - 1] = 0; m[:, 1::2, :, V - PH:V - 1] = 255; m[..., V - 1] = 255
    m[:, 1::2, :, lo] = 0; m[:, 1::2, :, hi] = 0; m[:, ::2, :, lo] = 255; m[:, ::2, :, hi] = 255
    u[:, 1::2, :, 0] = np.where(np.arange(16) % 2 == 0, 0, V - 1); b[:, 1::2, :, 0] = 0; d[:, 1::2, :, 0] = P - 1
    u[..., C - 1] = np.where(np.arange(16) % 2 == 0, hi, lo)
    b[..., lo] = 0; d[..., lo] = P - 1; b[..., hi] = P - 1; d[..., hi] = 0; d[..., V - 1] = 0
    b[:, :, 15, V - 1] = ((C - 1 - 97 * (PH - 1)) & (C - 1)) + P - C
    return pack(x, m, b, d, u)
def check_inputs(d):
    bad = []
    for k, hi in (("mor", 255), ("mea", 255), ("bas", P - 1), ("der", P - 1), ("use", V - 1)):
        a = np.asarray(d[k]).astype(np.float64)
        if not np.all((a >= 0) & (a <= hi) & (a == np.floor(a))): bad.append("range of " + k)
    return bad
def pick(a, ix):
    return np.stack([np.take(a[g], ix[g], axis=1) for g in range(8)])
def model(kap, mv, own, m, b, d, u):
    c = pick(u, kap)
    s = np.add.reduce(np.abs(pick(m, c) - mv[:, :, None, :]), axis=1)
    k = np.minimum.reduce(np.where(c == own, 2 ** 24, s * 2048 + c), axis=1)
    ok = k < 2 ** 24; w = np.where(ok, k & 2047, 0); dm = pick(d, w)
    diff = pick(b, w) != dm; diff[:, 15] = True
    return ok, w, np.argmax(diff, axis=1), dm
def gap(x, l, mv):
    return np.add.reduce(np.abs(np.maximum.reduce(pick(x, l), axis=2) - mv), axis=1)
def reference(mor, mea, bas, der, use):
    x = mor.astype(np.float32).astype(np.int32).reshape(N, 8, 16, P); m = mea.astype(np.float32).astype(np.int32).reshape(N, 8, 16, V)
    b = bas.astype(np.int32).reshape(N, 8, 16, V); d = der.astype(np.int32).reshape(N, 8, 16, V); u = use.astype(np.int32).reshape(N, 8, 16, C)
    row = np.arange(16)[None, :, None]; i = np.arange(I); count = [0] * N
    for t in range(RO):
        v = PH * i + t % PH; todo = []
        for r in range(N):
            mv = m[r][:, :, v]; bv = b[r][:, :, v]; dv = d[r][:, :, v]; kap = (bv[:, 15] + 97 * t) & (C - 1); mar = count[r] & 127
            ok, w, f, dm = model(kap, mv, v, m[r], b[r], d[r], u[r])
            e = np.where(row < f[:, None, :], bv, dm); old = gap(x[r], dv, mv)
            ad = ok & (gap(x[r], e, mv) + mar < old)
            q = (r + 1 + t % (N - 1)) % N
            sel = np.argsort(ad, axis=1, kind="stable")[:, :CAP]
            asks = ~np.take_along_axis(ad, sel, 1); mv2 = pick(mv, sel)
            ok2, w2, f2, dm2 = model(np.take_along_axis(kap, sel, 1), mv2, -1, m[q], b[q], d[q], u[q])
            e2 = np.where(row < f2[:, None, :], pick(bv, sel), dm2)
            ad2 = asks & (gap(x[r], e2, mv2) + mar < np.take_along_axis(old, sel, 1))
            new = np.where(ad[:, None, :], e, dv); got = ad.copy()
            for g in range(8):
                new[g][:, sel[g][ad2[g]]] = e2[g][:, ad2[g]]; got[g, sel[g][ad2[g]]] = True
            todo.append((ad, w, new, got, (np.add.reduce((row + 1) * mv, axis=1) + t) & (Z - 1)))
        for r in range(N):
            ad, w, new, got, z = todo[r]; d[r][:, :, v] = new; count[r] = int(np.count_nonzero(got))
            for g in range(8):
                j = i[ad[g]]; u[r, g, (j + t) & 15, (j + 37 * t) & (C - 1)] = w[g][j] ^ 1
                j = i[got[g]]; x[r, g][:, S * j + z[g][j]] = m[r, g][:, v[j]]
    return {"yd": d.reshape(N, 128, V).astype(np.float32), "yu": u.reshape(N, 128, C).astype(np.float32), "ym": x.reshape(N, 128, P).astype(np.float32).astype(BF)}

@@ -1,0 +1,543 @@
+from concourse.mybir import AluOpType as OP, AxisListType, ActivationFunctionType as AF
+
+S_, P_ = "sbuf", "psum"
+F, B, I, U = "float32", "bfloat16", "int32", "uint16"
+MO, MD, MX = 512, 2560, 4608
+SCRATCH = {}
+
+
+def _buf(names, n, d, where=S_):
+    for x in names.split():
+        SCRATCH[x] = (where, [128, n], d)
+
+
+_buf("b15", 994, I)
+_buf("basi deri usei", 1024, I)
+_buf("meas", 1024, B)
+_buf("morw", 4624, B)
+_buf("usef ydb", 1024, F)
+_buf("tl xr", 2048, F)
+_buf("mvt0 mvt1 got", 640, B)
+_buf("bst0 bst1 gds cq", 640, F)
+_buf("dri0 dri1 nd", 640, I)
+_buf("dro0 dro1 cdo eo", 512, U)
+_buf("rep0 rep1 dm gd", 8192, B)
+_buf("mq0 mq1 mq2", 1024, B)
+_buf("uq0 uq1 uq2 tq0 tq1 tq2", 1024, F)
+_buf("wi wj pi pk zi zt zu", 32, I)
+_buf("kap0 kap1 kap2 wo gu", 32, U)
+_buf("gf zw0 zw1 zc i16 iw", 32, F)
+_buf("cdf eq ks ec dk vr0 vr1 minm", 512, F)
+_buf("um us m8 m8r", 256, F)
+_buf("es rp2 rm zsp dg", 2048, B)
+_buf("one dd ee fail cum junk sg neq", 512, B)
+_buf("marg cn thr jp", 1, F)
+_buf("acc sm bj j2", 8, F)
+_buf("sel w2o", 8, U)
+_buf("c2f bs2 gd2 dr2 ks2 ec2 x2 ad2 y2 n2 id1 idb on", 128, F)
+_buf("c2o eo2", 128, U)
+_buf("mv2 ee2 b1 bm tri idh idn wz", 128, B)
+_buf("um2 us2", 64, F)
+_buf("g8", 8, B)
+_buf("la", 1024, F)
+_buf("kin", 528, I)
+_buf("km", 528, B)
+_buf("pK pU pG pD pC pM pX0 pX1", 512, F, P_)
+SEMAPHORES = ["cv", "cs", "cp", "cg"] + ["d%d" % i for i in range(24)] + ["rl%d" % i for i in range(9)] + ["ar%d" % i for i in range(9)]
+BIG = float(2 ** 25)
+EORD = ("G2 W0 W1 W2 W3 W4 G6 W5 W6 W7", "G3 W0 W1 W2 W3 G7 W4 W5 W6 W7", "G3 W0 W1 W2 W3 G7 W4 W5 W6 W7")
+DSPLIT = ("ssss", "sssv", "sssv")
+MSPLIT = ("pvvvvvvv", "vvvvpvvv", "vpvvvvvv")
+FILL = ((2, 1, 1, 2), (5, 2, 1, 2), (0, 0, 0, 0))
+DFILL = ((2, 2, 2), (0, 2, 1), (2, 2, 2))
+CNTV = (0, 0, 2)
+
+
+def rank_program(g, core, T, topo):
+    rank = T.rank_of(core)
+    if rank is None:
+        return
+    queue = {"v": g.vector, "s": g.scalar, "p": g.tensor, "g": g, "y": g.sync}
+    clock = {q: {} for q in queue}
+    total, log, nd = {}, {}, [0]
+
+    def X(name, lo=0, hi=None, st=None):
+        hi = SCRATCH[name][1][1] if hi is None else hi
+        return (T[name][:, lo:hi] if st is None else T[name][:, lo:hi:st], name, lo, hi)
+
+    def emit(q, fn, R, W, sem=None, n=1, tot=None):
+        deps = []
+        touch = [(v[1], v[2], v[3], False) for v in R] + [(v[1], v[2], v[3], True) for v in W]
+        for name, lo, hi, w in touch:
+            ps = SCRATCH[name][0] == "psum"
+            for rec in log.get(name, []):
+                if not ps and (rec[1] <= lo or hi <= rec[0]):
+                    continue
+                if not (w or rec[2] or ps):
+                    continue
+                if rec[3] == q and sem is None and rec[7]:
+                    if q == "p" or not (w or rec[2]) or rec[1] <= lo or hi <= rec[0]:
+                        continue
+                deps.append(rec)
+        for rec in sorted(deps, key=lambda r: -r[8]):
+            if clock[q].get(rec[4], 0) < rec[5]:
+                queue[q].wait_ge(T.sem[rec[4]], rec[5])
+                for s, c in rec[6].items():
+                    clock[q][s] = max(clock[q].get(s, 0), c)
+        comp = sem is None
+        s = {"v": "cv", "s": "cs", "p": "cp", "g": "cg"}[q] if comp else sem
+        ins = fn(queue[q])
+        if n:
+            ins.then_inc(T.sem[s], n)
+        total[s] = total.get(s, 0) + n if comp else (tot or n)
+        c = dict(clock[q])
+        c[s] = total[s]
+        nd[0] += 1
+        for name, lo, hi, w in touch:
+            recs = log.setdefault(name, [])
+            if w:
+                recs = [r for r in recs if not (lo <= r[0] and r[1] <= hi)]
+            else:
+                recs = [r for r in recs if not (r[3] == q and comp and r[7] and not r[2] and lo <= r[0] and r[1] <= hi)]
+            recs.append((lo, hi, w, q, s, total[s], c, comp, nd[0]))
+            log[name] = recs
+
+    nsem = [0]
+
+    def dma(q, out, in_, R=(), W=(), sem=None, tot=None):
+        if sem is None:
+            sem = "d%d" % nsem[0]
+            nsem[0] += 1
+        emit(q, lambda e: e.dma_start(out, in_), R, W, sem=sem, n=16, tot=tot or 16)
+
+    def ind(win, off):
+        return (win[0].indirect(off[0]), win, off)
+
+    def rd(*vs):
+        r = []
+        for v in vs:
+            r += [v[1], v[2]] if len(v) == 3 else [v]
+        return r
+
+    def tt(out, a, b, op):
+        emit("v", lambda e: e.tensor_tensor(out[0], a[0], b[0], op), rd(a, b), [out])
+
+    def ts(out, a, s1, op0, s2=None, op1=None):
+        R = rd(a) + ([s1] if isinstance(s1, tuple) else [])
+        k1 = s1[0] if isinstance(s1, tuple) else s1
+        if op1 is None:
+            emit("v", lambda e: e.tensor_scalar(out[0], a[0], k1, None, op0), R, [out])
+        else:
+            emit("v", lambda e: e.tensor_scalar(out[0], a[0], k1, s2, op0, op1), R, [out])
+
+    def cp(out, a):
+        if len(out) == 3:
+            emit("v", lambda e: e.tensor_copy(out[0], a[0]), rd(a) + [out[2]], [out[1]])
+        else:
+            emit("v", lambda e: e.tensor_copy(out[0], a[0]), rd(a), [out])
+
+    def ms(out, val):
+        emit("v", lambda e: e.memset(out[0], val), [], [out])
+
+    def red(out, a):
+        emit("v", lambda e: e.tensor_reduce(out[0], a[0], AxisListType.X, OP.add), [a], [out])
+
+    def scan(out, d0, d1, init, op0, op1):
+        emit("v", lambda e: e.tensor_tensor_scan(out[0], d0[0], d1[0], init, op0, op1), [d0, d1], [out])
+
+    def act(out, a, func, bias=0.0, scale=1.0, accum=None):
+        R = rd(a) + ([bias] if isinstance(bias, tuple) else [])
+        k = bias[0] if isinstance(bias, tuple) else bias
+        if accum:
+            emit("s", lambda e: e.activation(out[0], a[0], func, bias=k, scale=scale, accum_out=accum[0]), R, [out, accum])
+        else:
+            emit("s", lambda e: e.activation(out[0], a[0], func, bias=k, scale=scale), R, [out])
+
+    def mm(out, l, r, start, stop):
+        emit("p", lambda e: e.matmul(out[0], l[0], r[0], start, stop), [l, r], [out])
+
+    def iota(out, pat, base, cm, flt):
+        emit("g", lambda e: e.iota(out[0], pat, base, cm, allow_small_or_imprecise_dtypes=True) if flt else e.iota(out[0], pat, base, cm), [], [out])
+
+    def asel(b, pat, op, base, cm):
+        emit("g", lambda e: e.affine_select(b[0], b[0], pat, op, 0.0, base, cm), [b], [b])
+
+    cores = T.cores
+
+    def send(src, dst, t, ix):
+        to = cores[(rank - 1 - t) % len(cores)]
+        e = topo.engines(core, to)[:8]
+        m = sum(1 << k for k in e)
+        a = topo.addr(to)
+        out = T[dst][:, 0:1024]
+        emit("g", lambda q: q.remote_dma(out, src[0], T.sem["ar%d" % ix], T.sem["rl%d" % ix], a[1], a[0], m), [src], [], sem="rl%d" % ix, n=0, tot=len(e))
+        log.setdefault(dst, []).append((0, 1024, True, "x", "ar%d" % ix, len(e), {"ar%d" % ix: len(e)}, False, 0))
+        total["ar%d" % ix] = len(e)
+
+    dma("y", T.meas[:], T.mea[:], W=[X("meas")], sem="d1")
+    for b in range(16):
+        dma("y" if b % 2 == 0 else "s", T.b15[b::16, 0:994], T.bas[15::16, 2 * b:2 * b + 994], W=[X("b15")] if b == 15 else [], sem="d0", tot=256)
+    nsem[0] = 2
+    dma("s", T.usei[:], T.use[:], W=[X("usei")])
+    dma("y", T.deri[:], T.der[:], W=[X("deri")])
+    dma("s", T.morw[:, MO:MD], T.mor[:], W=[X("morw", MO, MD)])
+    dma("y", T.basi[:], T.bas[:], W=[X("basi")])
+    dma("y", T.morw[:, MD:MX], T.mor[:], W=[X("morw", MD, MX)])
+
+    def same(b, o, st):
+        asel(b, o + [[-16, 8]] + st, OP.is_ge, 0, 1)
+        asel(b, o + [[16, 8]] + st, OP.is_ge, 15, -1)
+
+    ms(X("rm"), 1.0)
+    ms(X("zsp"), 0.0)
+    ms(X("rm", 0, 2048, 16), 0.0)
+    ms(X("g8"), 2048.0)
+    ms(X("id1"), 1.0)
+    ms(X("idb"), float(2 ** 23 + 1024))
+    ms(X("mvt0", 512, 640), 0.0)
+    ms(X("idh"), 1.0)
+    ms(X("idn"), -1.0)
+    ms(X("minm"), 0.0)
+    ms(X("la"), 1.0)
+    ms(X("minm", 0, 512, 16), BIG)
+    ms(X("m8"), 1.0)
+    ms(X("b1"), 1.0)
+    same(X("g8"), [], [])
+    for n in ("id1", "idb", "idh", "idn"):
+        asel(X(n), [[-1, 128]], OP.is_equal, 0, 1)
+    iota(X("vr0"), [[2, 512]], 0, 0, True)
+    iota(X("pi"), [[0, 32]], 0, 1, False)
+    send(X("meas"), "mq0", 0, 0)
+    asel(X("la"), [[-16, 8], [0, 8], [-1, 16]], OP.is_equal, 0, 1)
+    same(X("m8"), [[0, 32]], [])
+    same(X("b1"), [], [[0, 16]])
+    iota(X("i16"), [[16, 32]], 0, 0, True)
+    iota(X("kin"), [[-1, 528]], 1024, 1, False)
+
+    def kap(t):
+        ts(X("zt"), X("b15", t % 2, 994, 32), 97 * t, OP.add)
+        ts(X("zu"), X("zt"), 1023, OP.bitwise_and)
+        cp(X("kap%d" % t), X("zu"))
+
+    def prep(t):
+        cp(X("cdf"), ind(X("usef") if t else X("usei"), X("kap%d" % t)))
+        cp(X("cdo"), X("cdf"))
+        tt(X("eq"), X("cdf"), X("vr%d" % (t % 2)), OP.is_equal)
+
+    late = []
+
+    def sub_abs(name, lo, rep, rlo):
+        for h in range(2):
+            a = X(name, lo + 512 * h, lo + 512 * h + 512)
+            mm(X("pX%d" % h), X("idh"), a, True, False)
+            mm(X("pX%d" % h), X("idn"), X(rep, rlo + 512 * h, rlo + 512 * h + 512), False, True)
+        for h in range(2):
+            act(X(name, lo + 512 * h, lo + 512 * h + 512), X("pX%d" % h), AF.Abs)
+
+    def chunk(t, c):
+        sl = X("dm", 1024 * c, 1024 * c + 1024)
+        rep = "rep%d" % (t % 2)
+        src = ind(X("meas"), X("cdo", 64 * c, 64 * c + 64))
+        if MSPLIT[t][c] == "v":
+            tt(sl, src, X(rep, 1024 * c, 1024 * c + 1024), OP.subtract)
+            act(sl, sl, AF.Abs)
+        else:
+            act(sl, src, AF.Copy)
+            sub_abs("dm", 1024 * c, rep, 1024 * c)
+        if c % 2:
+            late.append(c // 2)
+
+    def flush():
+        while late:
+            j = late.pop(0)
+            blk = X("pK", 128 * j, 128 * j + 128)
+            mm(blk, X("cdf", 128 * j, 128 * j + 128), X("id1"), True, False)
+            mm(blk, X("eq", 128 * j, 128 * j + 128), X("idb"), False, False)
+            for k in range(16):
+                mm(X("pK", 128 * j + k, 128 * j + 128, 16), X("dm", 2048 * j + k, 2048 * j + 2048, 16), X("g8"), False, k == 15)
+
+    done = {0: 0, 1: 0, 2: 0, 3: 8}
+
+    def fill(t, n):
+        for _ in range(n):
+            flush()
+            if done[t] < 8:
+                chunk(t, done[t])
+                done[t] += 1
+
+    def lists(c, offs, who, base, n):
+        src = ind(X("morw", MO, 4624) if base else X("morw", MO, MD), X(offs, n * c // 16, n * c // 16 + n // 16))
+        out = X("gd", n * c, n * c + n)
+        if who == "s":
+            act(out, src, AF.Copy)
+        else:
+            cp(out, src)
+
+    flip = [0]
+
+    def wide(c, dist, mv, n=1024):
+        lo = (c % (2048 // n)) * n
+        w = n // 16
+        scan(X("es", lo, lo + n), X("rm", 0, n), X("gd", n * c, n * c + n), 0.0, OP.mult, OP.max)
+        flip[0] ^= 1
+        px = X("pX%d" % flip[0], 0, w)
+        mm(px, X("idh"), X("es", lo + 15, lo + n, 16), True, False)
+        mm(px, X("idn"), X(mv, w * c, w * c + w), False, True)
+        act(X(dist, w * c, w * c + w), px, AF.Abs)
+
+    def tl_a(par):
+        tt(X("neq"), X("dri%d" % par, 0, 512), X("basi", par, 1024, 2), OP.not_equal)
+        mm(X("pC"), X("tri"), X("neq"), True, True)
+        act(X("sg"), X("pC"), AF.Sign, bias=X("thr"))
+        act(X("pC"), X("sg"), AF.Copy, bias=2048.0, scale=2048.0)
+
+    def tl_b(par):
+        tt(X("tl", par, 1024, 2), X("pC"), X("dri%d" % par, 0, 512), OP.add)
+
+    def z_tab(par):
+        mm(X("pM"), X("wz"), X("mvt%d" % par, 0, 512), True, True)
+        cp(X("kin", 0, 512), X("pM"))
+        ts(X("kin", 0, 512), X("kin", 0, 512), 3, OP.bitwise_and)
+        cp(X("junk"), X("kin", 0, 512))
+        for b in range(16):
+            mm(X("pU", 256, 288), X("dg", 128 * b, 128 * b + 128), X("junk", b, 512, 16), b == 0, b == 15)
+        cp(X("zw%d" % par), X("pU", 256, 288))
+
+    cp(X("mvt0", 0, 512), X("meas", 0, 1024, 2))
+    for k in range(16):
+        act(X("rep0", 4096 + k, 8192, 16), X("mvt0", 256, 512), AF.Copy)
+    for c in range(2):
+        cp(X("zsp", 0, 2048, 16), X("mvt0", 128 * c, 128 * c + 128))
+        scan(X("rep0", 2048 * c, 2048 * c + 2048), X("rm"), X("zsp"), 0.0, OP.mult, OP.add)
+    kap(0)
+    prep(0)
+    fill(0, 1)
+    cp(X("dri0", 0, 512), X("deri", 0, 1024, 2))
+    cp(X("dro0"), X("dri0", 0, 512))
+    fill(0, 1)
+    ms(X("bm"), -1.0)
+    ms(X("one"), 1.0)
+    ms(X("tri"), 1.0)
+    ms(X("dri0", 512, 640), 0)
+    ms(X("dri1", 512, 640), 0)
+    ms(X("nd", 512, 640), 0)
+    ms(X("mvt1", 512, 640), 0.0)
+    cp(X("mvt1", 0, 512), X("meas", 1, 1024, 2))
+    same(X("bm"), [], [[0, 16]])
+    iota(X("tl", 1024, 2048), [[0, 1024]], 6144, 0, True)
+    same(X("tri"), [], [[0, 16]])
+    asel(X("tri"), [[1, 128]], OP.is_ge, 0, -1)
+    for k in range(16):
+        emit("g", lambda e: e.affine_select(T.rep1[:, k:8192:16], T.mvt1[:, 0:512], [[0, 512]], OP.is_ge, 0.0, 1, 0), [X("mvt1", 0, 512)],
+             [X("rep1")] if k == 15 else [])
+
+    def setup_0():
+        ts(X("pk"), X("pi"), 15, OP.bitwise_and)
+        ts(X("thr"), X("pk", 0, 1), 15, OP.is_ge, 1.5, OP.mult)
+        ts(X("thr"), X("thr"), -0.5, OP.add)
+        tl_a(0)
+        cp(X("dri1", 0, 512), X("deri", 1, 1024, 2))
+        ms(X("m8r"), 1.0)
+        ms(X("m8r", 0, 256, 8), 0.0)
+
+    def setup_1():
+        cp(X("usef"), X("usei"))
+        send(X("usef"), "uq0", 0, 1)
+        tl_b(0)
+        tl_a(1)
+
+    def setup_a():
+        for par in range(2):
+            ts(X("bst%d" % par, 0, 512), X("basi", par, 1024, 2), 2048.0, OP.add)
+            ms(X("bst%d" % par, 512, 640), 2048.0)
+        ms(X("morw", MX, 4624), 16384.0)
+        ms(X("marg"), 0.0)
+        ms(X("on"), 1.0)
+        tl_b(1)
+        tt(X("iw"), X("pk"), X("i16"), OP.add)
+        ts(X("bj"), X("iw", 0, 8), 0.5, OP.add)
+        ts(X("j2"), X("iw", 0, 8), 2.0, OP.mult)
+        send(X("tl", 0, 1024), "tq0", 0, 2)
+        iota(X("xr"), [[2, 1024], [-1, 2]], 1, 0, True)
+        iota(X("vr1"), [[2, 512]], 1, 0, True)
+        iota(X("dg"), [[0, 2048]], 1, 0, True)
+        asel(X("dg"), [[0, 16], [-16, 8], [-1, 16]], OP.is_equal, 0, 1)
+        asel(X("dg"), [[-1, 16], [0, 8], [1, 16]], OP.is_equal, 0, 0)
+        send(X("meas"), "mq1", 1, 3)
+        send(X("meas"), "mq2", 2, 6)
+
+    def setup_b():
+        ms(X("gds", 512, 640), -100000.0)
+        ms(X("got", 512, 640), 0.0)
+        ms(X("cq", 512, 640), 0.0)
+        ts(X("kin"), X("kin"), 15, OP.bitwise_and)
+        ts(X("km"), X("kin"), 0, OP.is_equal)
+        kap(1)
+        kap(2)
+
+    def setup_c():
+        cp(X("dro1"), X("dri1", 0, 512))
+        ts(X("jp"), X("pk", 0, 1), 1.0, OP.add)
+        ts(X("wz"), X("b1"), X("jp"), OP.mult)
+        z_tab(0)
+        z_tab(1)
+
+    for t in range(3):
+        par = t % 2
+        mvt, bst, dri = "mvt%d" % par, "bst%d" % par, "dri%d" % par
+        for c in range(4):
+            lists(c, "dro%d" % par, DSPLIT[t][c], 0, 2048)
+            if t and c == 0:
+                tl_a(1 - par)
+            fill(t, DFILL[t][c] if c < 3 else 8)
+            if t == 0 and c < 3:
+                (setup_0, setup_1, setup_a)[c]()
+            if t and c == 1:
+                tl_b(1 - par)
+                send(X("tl", 0, 1024), "tq%d" % t, t, 5 if t == 1 else 8)
+            if 1 <= c < 3:
+                wide(c - 1, "dd", mvt, 2048)
+        flush()
+        scan(X("ks"), X("minm"), X("pK"), BIG, OP.max, OP.min)
+        for a in range(8):
+            mm(X("pU", 32 * a, 32 * a + 32), X("la", 128 * a, 128 * a + 128), X("ks", 15, 512, 16), True, True)
+        wide(2, "dd", mvt, 2048)
+        tt(X("um"), X("pU", 0, 256), X("m8"), OP.mult)
+        wide(3, "dd", mvt, 2048)
+        mm(X("pD"), X("b1"), X("dd"), True, True)
+        mm(X("pG"), X("bm"), X("dd"), True, False)
+        scan(X("us"), X("m8r"), X("um"), 0.0, OP.mult, OP.add)
+        mine = [c for c in range(8) if "G%d" % c not in EORD[t]]
+        ahead = []
+
+        def gather_e(n, top):
+            for c in [c for c in mine if c not in ahead and c < top][:n]:
+                lists(c, "eo", "s", 1, 1024)
+                ahead.append(c)
+
+        for h in range(2):
+            for j in (2 * h, 2 * h + 1):
+                cp(X("wi", 8 * j, 8 * j + 8), X("us", 8 * j + 7, 256, 32))
+            w = (16 * h, 16 * h + 16)
+            ts(X("wj", *w), X("wi", *w), 2047, OP.bitwise_and)
+            cp(X("wo", *w), X("wj", *w))
+            l = (256 * h, 256 * h + 256)
+            tt(X("ec", *l), ind(X("tl"), X("wo", *w)), X(bst, *l), OP.max)
+            ts(X("eo", *l), X("ec", *l), -2048.0, OP.add)
+            if h == 0:
+                gather_e(4, 4)
+        if t == 0:
+            setup_b()
+        us = X("usef", 37 * t, 37 * t + 512)
+        gather_e(4 - len(ahead), 8)
+        for tok in EORD[t].split():
+            c = int(tok[1])
+            if tok[0] == "G":
+                lists(c, "eo", "v", 1, 1024)
+                continue
+            gather_e(1, 8)
+            wide(c, "ee", mvt)
+            if c == 2:
+                cp(X("dk"), ind(X("xr"), X("wo")))
+            if c == 4:
+                tt(X("pM"), X("dk"), us, OP.subtract)
+                tt(X("dk"), X("pM"), X("km", t, t + 512), OP.mult)
+        mm(X("pG"), X("b1"), X("ee"), False, True)
+        ts(X("fail"), X("pG"), X("marg"), OP.add, 0.0, OP.is_ge)
+        scan(X("cum"), X("fail"), X("fail"), 0.0, OP.add, OP.max)
+        for a in range(8 - CNTV[t]):
+            act(X("junk"), X("cum"), AF.Sign, bias=X("bj", a, a + 1), scale=-1.0, accum=X("acc", a, a + 1))
+        act(X("cq", 0, 512), ind(X("uq%d" % t), X("kap%d" % t)), AF.Copy)
+        act(X("gds", 0, 512), X("pD"), AF.Copy)
+        act(X("got", 0, 512), X("fail"), AF.Copy, bias=1.0, scale=-1.0)
+        mm(X("pC"), X("idn"), X("fail"), True, False)
+        mm(X("pC"), X("idh"), X("one"), False, True)
+        tt(X("pM"), X("dk"), X("pC"), OP.mult)
+        tt(us, X("pM"), us, OP.add)
+        if t < 2:
+            send(X("usef"), "uq%d" % (t + 1), t + 1, 4 if t == 0 else 7)
+            prep(t + 1)
+        else:
+            dma("y", T.yu[:], T.usef[:], R=[X("usef")])
+        tt(X("pM"), X("ec"), X("pC"), OP.mult)
+        tt(X("nd", 0, 512), X("pM"), X(dri, 0, 512), OP.max)
+        for a in range(8 - CNTV[t], 8):
+            ts(X("neq"), X("cum"), X("bj", a, a + 1), OP.is_le)
+            red(X("acc", a, a + 1), X("neq"))
+            ts(X("acc", a, a + 1), X("acc", a, a + 1), 2.0, OP.mult, -512.0, OP.add)
+        if t == 0:
+            setup_c()
+        fill(t + 1, FILL[t][0])
+        ts(X("sm"), X("acc"), 511.0, OP.is_gt)
+        tt(X("sm"), X("sm"), X("j2"), OP.mult)
+        tt(X("sm"), X("sm"), X("acc"), OP.add)
+        ts(X("sel"), X("sm"), 0.5, OP.mult, 256.0, OP.add)
+        cp(X("c2f"), ind(X("cq"), X("sel")))
+        cp(X("c2o"), X("c2f"))
+        cp(X("mv2"), ind(X(mvt), X("sel")))
+        cp(X("zsp", 0, 2048, 16), X("mv2"))
+        scan(X("rp2"), X("rm"), X("zsp"), 0.0, OP.mult, OP.add)
+        mm(X("pC", 0, 128), X("c2f"), X("id1"), True, False)
+        act(X("gd", 5120, 6144), ind(X("mq%d" % t), X("c2o", 64, 128)), AF.Copy)
+        tt(X("gd", 4096, 5120), ind(X("mq%d" % t), X("c2o", 0, 64)), X("rp2", 0, 1024), OP.subtract)
+        sub_abs("gd", 5120, "rp2", 1024)
+        act(X("gd", 4096, 5120), X("gd", 4096, 5120), AF.Abs)
+        for k in range(16):
+            mm(X("pC", k, 128, 16), X("gd", 4096 + k, 6144, 16), X("g8"), False, k == 15)
+        act(X("gd2"), ind(X("gds"), X("sel")), AF.Copy)
+        cp(X("bs2"), ind(X(bst), X("sel")))
+        cp(X("dr2"), ind(X(dri), X("sel")))
+        fill(t + 1, FILL[t][1])
+        scan(X("ks2"), X("minm", 0, 128), X("pC", 0, 128), BIG, OP.max, OP.min)
+        for a in range(8):
+            mm(X("pU", 8 * a, 8 * a + 8), X("la", 128 * a, 128 * a + 128), X("ks2", 15, 128, 16), True, True)
+        fill(t + 1, FILL[t][2])
+        tt(X("um2"), X("pU", 0, 64), X("m8", 0, 64), OP.mult)
+        scan(X("us2"), X("m8r", 0, 64), X("um2"), 0.0, OP.mult, OP.add)
+        cp(X("wi", 0, 8), X("us2", 7, 64, 8))
+        ts(X("wj", 0, 8), X("wi", 0, 8), 2047, OP.bitwise_and)
+        cp(X("w2o"), X("wj", 0, 8))
+        tt(X("ec2"), ind(X("tq%d" % t), X("w2o")), X("bs2"), OP.max)
+        ts(X("eo2"), X("ec2"), -2048.0, OP.add)
+        lists(0, "eo2", "s", 1, 1024)
+        lists(1, "eo2", "v", 1, 1024)
+        wide(0, "ee2", "mv2")
+        wide(1, "ee2", "mv2")
+        mm(X("pD", 0, 128), X("b1"), X("ee2"), True, True)
+        cp(X("zi"), X("zw%d" % par))
+        ts(X("zt"), X("zi"), t, OP.add)
+        ts(X("zu"), X("zt"), 3, OP.bitwise_and)
+        ts(X("zc"), X("iw"), 3.0, OP.mult, float(MO), OP.add)
+        tt(X("zc"), X("zc"), X("zu"), OP.add)
+        fill(t + 1, FILL[t][3])
+        tt(X("x2"), X("pD", 0, 128), X("gd2"), OP.subtract)
+        ts(X("ad2"), X("x2"), X("marg"), OP.add, 0.0, OP.is_lt)
+        cp(ind(X("got"), X("sel")), X("ad2"))
+        for b in range(16):
+            mm(X("pU", 256, 288), X("dg", 128 * b, 128 * b + 128), X("got", b, 512, 16), b == 0, b == 15)
+        tt(X("y2"), X("ad2"), X("ec2"), OP.mult)
+        tt(X("n2"), X("y2"), X("dr2"), OP.max)
+        tt(X("gf"), X("pU", 256, 288), X("zc"), OP.mult)
+        tt(X("gf"), X("gf"), X("iw"), OP.add)
+        cp(X("gu"), X("gf"))
+        cp(ind(X("morw", 0, MD), X("gu")), X(mvt, 0, 512))
+        if t < 2:
+            red(X("cn"), X("pU", 256, 288))
+            mm(X("pC", 0, 1), X("on"), X("cn"), True, True)
+            dma("y", T.morw[:, MD:MX], T.morw[:, MO:MD], R=[X("morw", MO, MD)], W=[X("morw", MD, MX)])
+        else:
+            dma("s", T.ym[:], T.morw[:, MO:MD], R=[X("morw", MO, MD)])
+        cp(ind(X("nd"), X("sel")), X("n2"))
+        ts(X(dri), X("nd"), 2047, OP.bitwise_and)
+        if t < 2:
+            cp(X("wi", 0, 1), X("pC", 0, 1))
+            ts(X("wj", 0, 1), X("wi", 0, 1), 127, OP.bitwise_and)
+            cp(X("marg"), X("wj", 0, 1))
+            if t == 0:
+                cp(X("dro0"), X("dri0", 0, 512))
+        if t > 0:
+            cp(X("ydb", par, 1024, 2), X(dri, 0, 512))
+    dma("y", T.yd[:], T.ydb[:], R=[X("ydb")])
+    for s in sorted(total):
+        if clock["g"].get(s, 0) < total[s]:
+            g.wait_ge(T.sem[s], total[s])

@@ -1,114 +1,204 @@
 from concourse.mybir import AluOpType as OP, AxisListType, ActivationFunctionType as AF
 
 S_, P_ = "sbuf", "psum"
-F, B, I, U = "float32", "bfloat16", "int32", "uint16"
-MO, MD, MX = 512, 2560, 4608
-SCRATCH = {}
+F, B, H, I, U = "float32", "bfloat16", "float16", "int32", "uint16"
+FAR = 2048
+SH = 2064
+E0, D0 = 1024, 1536
+SCRATCH, PART = {}, {}
 
 
 def _buf(names, n, d, where=S_):
     for x in names.split():
-        SCRATCH[x] = (where, [128, n], d)
+        if n > 100:
+            SCRATCH[x] = (where, [128, n], d)
+            PART[x] = (x, 0, n)
+        else:
+            home = "small_" + d
+            at = SCRATCH[home][1][1] if home in SCRATCH else 0
+            SCRATCH[home] = (where, [128, at + (n + 15) // 16 * 16], d)
+            PART[x] = (home, at, n)
 
 
+_buf("bw", 128, I)
 _buf("b15", 994, I)
-_buf("basi deri usei", 1024, I)
-_buf("meas", 1024, B)
-_buf("morw", 4624, B)
-_buf("usef ydb", 1024, F)
-_buf("tl xr", 2048, F)
-_buf("mvt0 mvt1 got", 640, B)
-_buf("bst0 bst1 gds cq", 640, F)
-_buf("dri0 dri1 nd", 640, I)
+_buf("basi usei uq0 uq1 uq2", 1024, I)
+_buf("dt", 2816, I)
+_buf("meas mq0 mq1 mq2 rm zsp la1 la2", 1024, B)
+_buf("mor0 mor1", 4624, B)
+_buf("usef tq0 tq1 tq2", 1024, F)
+_buf("tl", 1032, F)
+_buf("ydb", 2560, F)
+_buf("mvt0 mvt1 dd", 640, B)
+_buf("mvp0 mvp1 mpt0 mpt1 eq ee neq minm vrh vrl0 vrl1 oner", 512, B)
+_buf("bst0 bst1 cq", 640, F)
 _buf("dro0 dro1 cdo eo", 512, U)
-_buf("rep0 rep1 dm gd", 8192, B)
-_buf("mq0 mq1 mq2", 1024, B)
-_buf("uq0 uq1 uq2 tq0 tq1 tq2", 1024, F)
-_buf("wi wj pi pk zi zt zu", 32, I)
-_buf("kap0 kap1 kap2 wo gu", 32, U)
-_buf("gf zw0 zw1 zc i16 iw", 32, F)
-_buf("cdf eq ks ec dk vr0 vr1 minm", 512, F)
-_buf("um us m8 m8r", 256, F)
-_buf("es rp2 rm zsp dg", 2048, B)
-_buf("one dd ee fail cum junk sg neq", 512, B)
-_buf("marg cn thr jp", 1, F)
-_buf("acc sm bj j2", 8, F)
-_buf("sel w2o", 8, U)
-_buf("c2f bs2 gd2 dr2 ks2 ec2 x2 ad2 y2 n2 id1 idb on", 128, F)
+_buf("rep0 rep1", 6144, B)
+_buf("es", 4096, B)
+_buf("bsh0 bsh1", 512, H)
+_buf("junk", 256, B)
+_buf("dm gd", 8192, B)
+_buf("g2 xp", 2048, B)
+_buf("dg", 2080, B)
+_buf("cdf ks", 512, F)
+_buf("ec", 512, I)
+_buf("zs", 512, H)
+_buf("u16", 592, H)
+_buf("um", 256, H)
+_buf("us", 256, F)
+_buf("m8 m8r", 256, B)
+_buf("ia ib ic pi", 32, I)
+_buf("ja jb jc", 8, I)
+_buf("kap", 192, U)
+_buf("wo po0 po1 ua ub", 32, U)
+_buf("sel blk w2o uc ud", 8, U)
+_buf("iw i16 wf fa fb fc bc", 32, F)
+_buf("zw", 64, F)
+_buf("old tgt dpos epos", 96, F)
+_buf("cumw sum", 40, F)
+_buf("fw", 40, B)
+_buf("gw", 32, B)
+_buf("mh dw vw", 32, H)
+_buf("col", 8, F)
+_buf("acc bj ga gb sf tg2 pd2 f2m f2d", 8, F)
+_buf("c2f bs2 id1 srow", 128, F)
+_buf("ec2 ea2", 128, I)
 _buf("c2o eo2", 128, U)
-_buf("mv2 ee2 b1 bm tri idh idn wz", 128, B)
-_buf("um2 us2", 64, F)
+_buf("mv2 mt2 dd2 ee2 cmp b1 tri ust idh idn idb one c4k", 128, B)
+_buf("zs2", 128, H)
+_buf("m0p m0n", 144, B)
 _buf("g8", 8, B)
-_buf("la", 1024, F)
-_buf("kin", 528, I)
-_buf("km", 528, B)
-_buf("pK pU pG pD pC pM pX0 pX1", 512, F, P_)
-SEMAPHORES = ["cv", "cs", "cp", "cg"] + ["d%d" % i for i in range(24)] + ["rl%d" % i for i in range(9)] + ["ar%d" % i for i in range(9)]
+_buf("pK pX0 pX1 pG pS pU pB pF", 512, F, P_)
+SEMAPHORES = ["cv", "cs", "cp", "cg"] + ["d%d" % i for i in range(40)] + ["rl%d" % i for i in range(9)] + ["ar%d" % i for i in range(9)]
 BIG = float(2 ** 25)
-EORD = ("G2 W0 W1 W2 W3 W4 G6 W5 W6 W7", "G3 W0 W1 W2 W3 G7 W4 W5 W6 W7", "G3 W0 W1 W2 W3 G7 W4 W5 W6 W7")
-DSPLIT = ("ssss", "sssv", "sssv")
-MSPLIT = ("pvvvvvvv", "vvvvpvvv", "vpvvvvvv")
-FILL = ((2, 1, 1, 2), (5, 2, 1, 2), (0, 0, 0, 0))
-DFILL = ((2, 2, 2), (0, 2, 1), (2, 2, 2))
-CNTV = (0, 0, 2)
+SIZE = {F: 4, I: 4, B: 2, H: 2, U: 2}
+SEARCH = ("vvvvswwswwswwsww", "vvvvvvvvvvvvssss", "vvvvvvvvvvvvssss")
+KEYS = ((0, 1, 2, 3), (0, 3, 1, 2), (0, 3, 1, 2))
+ASK = "vsvv"
+REP = 6144
+DWHO = ("ssssssss", "ssssssss", "ssssssss")
+EWHO = ("svsvsvss", "svsvsvss", "svsvsvss")
+CY, GAT, SCA, HOP = 0.00092, 1.5, 3.5, 0.1
+ORDER = []
+PASSES = 4
+
+
+def arrange(ops):
+    n = len(ops)
+    fwd, bwd = [[] for _ in ops], [[] for _ in ops]
+    for j, o in enumerate(ops):
+        for i, wait in o["deps"].items():
+            gap = ops[i]["lat"] + HOP if wait else 0.0
+            fwd[i].append((j, gap))
+            bwd[j].append((i, gap))
+
+    def place(nxt, prv, rank, first):
+        left = [len(p) for p in prv]
+        ready = list(first)
+        free, pool = {}, {}
+        for i, o in enumerate(ops):
+            free[o["q"]] = 0.0
+            pool.setdefault(o["q"], [])
+            if not left[i]:
+                pool[o["q"]].append(i)
+        order, end, pick = [], [0.0] * n, {}
+        while len(order) < n:
+            for q in pool:
+                if pool[q] and q not in pick:
+                    now = max(free[q], min(ready[i] for i in pool[q]))
+                    top = max(pool[q], key=lambda i: (ready[i] <= now, rank[i], -i))
+                    c = ops[top]["cost"]
+                    soon = [i for i in pool[q] if now < ready[i] <= now + 0.5 * c and rank[i] > rank[top] + c]
+                    if soon:
+                        top = max(soon, key=lambda i: rank[i])
+                        now = ready[top]
+                    pick[q] = (now, top)
+            now, i = min(pick.values())
+            q = ops[i]["q"]
+            del pick[q]
+            pool[q].remove(i)
+            end[i] = free[q] = now + ops[i]["cost"]
+            order.append(i)
+            for j, gap in nxt[i]:
+                ready[j] = max(ready[j], end[i] + gap)
+                left[j] -= 1
+                if not left[j]:
+                    pool[ops[j]["q"]].append(j)
+                    pick.pop(ops[j]["q"], None)
+        return order, end
+
+    tail = [o["lat"] for o in ops]
+    rank = [0.0] * n
+    for i in range(n - 1, -1, -1):
+        rank[i] = ops[i]["cost"] + max([tail[i]] + [rank[j] + gap for j, gap in fwd[i]])
+    best = None
+    for _ in range(PASSES):
+        order, end = place(fwd, bwd, rank, [0.0] * n)
+        span = max(e + t for e, t in zip(end, tail))
+        if best is None or span < best[0]:
+            best = (span, order)
+        rank = place(bwd, fwd, end, tail)[1]
+    return best[1]
 
 
 def rank_program(g, core, T, topo):
     rank = T.rank_of(core)
     if rank is None:
         return
-    queue = {"v": g.vector, "s": g.scalar, "p": g.tensor, "g": g, "y": g.sync}
-    clock = {q: {} for q in queue}
-    total, log, nd = {}, {}, [0]
+    ops, log = [], {}
 
-    def X(name, lo=0, hi=None, st=None):
+    def X(name, lo=0, hi=None, st=1):
+        name, at, n = PART[name]
+        lo, hi = at + lo, at + (n if hi is None else hi)
+        return (T[name][:, lo:hi] if st == 1 else T[name][:, lo:hi:st], name, lo, hi, st)
+
+    def X0(name, lo=0, hi=None):
         hi = SCRATCH[name][1][1] if hi is None else hi
-        return (T[name][:, lo:hi] if st is None else T[name][:, lo:hi:st], name, lo, hi)
+        return (T[name][0:1, lo:hi], name, lo, hi, 1)
 
-    def emit(q, fn, R, W, sem=None, n=1, tot=None):
-        deps = []
-        touch = [(v[1], v[2], v[3], False) for v in R] + [(v[1], v[2], v[3], True) for v in W]
-        for name, lo, hi, w in touch:
-            ps = SCRATCH[name][0] == "psum"
-            for rec in log.get(name, []):
-                if not ps and (rec[1] <= lo or hi <= rec[0]):
-                    continue
-                if not (w or rec[2] or ps):
-                    continue
-                if rec[3] == q and sem is None and rec[7]:
-                    if q == "p" or not (w or rec[2]) or rec[1] <= lo or hi <= rec[0]:
-                        continue
-                deps.append(rec)
-        for rec in sorted(deps, key=lambda r: -r[8]):
-            if clock[q].get(rec[4], 0) < rec[5]:
-                queue[q].wait_ge(T.sem[rec[4]], rec[5])
-                for s, c in rec[6].items():
-                    clock[q][s] = max(clock[q].get(s, 0), c)
+    def cnt(v):
+        return 16 * cnt(v[2]) if len(v) == 3 else len(range(v[2], v[3], v[4]))
+
+    def meet(a, lo, hi, st):
+        if a[1] <= lo or hi <= a[0]:
+            return False
+        return not (st > 1 and a[2] == st and (a[0] - lo) % st)
+
+    def emit(q, fn, R, W, cost, sem=None, n=1, tot=None, lat=0.0, after=()):
+        me = len(ops)
         comp = sem is None
-        s = {"v": "cv", "s": "cs", "p": "cp", "g": "cg"}[q] if comp else sem
-        ins = fn(queue[q])
-        if n:
-            ins.then_inc(T.sem[s], n)
-        total[s] = total.get(s, 0) + n if comp else (tot or n)
-        c = dict(clock[q])
-        c[s] = total[s]
-        nd[0] += 1
-        for name, lo, hi, w in touch:
+        deps = {d: False for d in after}
+        touch = [(v[1], v[2], v[3], v[4] if comp else 1, False) for v in R] + [(v[1], v[2], v[3], v[4] if comp else 1, True) for v in W]
+        for name, lo, hi, st, w in touch:
+            ps = SCRATCH[name][0] == P_
+            for rec in log.get(name, []):
+                o = ops[rec[4]]
+                same = comp and o["comp"] and o["q"] == q
+                if ps and same and q == "p":
+                    deps.setdefault(rec[4], False)
+                elif ps and not same:
+                    deps[rec[4]] = True
+                elif (w or rec[3]) and meet(rec, lo, hi, st if o["comp"] else 1):
+                    deps[rec[4]] = True
+        ops.append(dict(q=q, fn=fn, cost=cost, lat=lat, deps=deps, comp=comp, sem=sem, n=n, tot=tot))
+        for name, lo, hi, st, w in touch:
             recs = log.setdefault(name, [])
-            if w:
+            if SCRATCH[name][0] == P_:
+                recs = [r for r in recs if q != "p" and (r[3] or ops[r[4]]["q"] == q)]
+            if w and st == 1:
                 recs = [r for r in recs if not (lo <= r[0] and r[1] <= hi)]
-            else:
-                recs = [r for r in recs if not (r[3] == q and comp and r[7] and not r[2] and lo <= r[0] and r[1] <= hi)]
-            recs.append((lo, hi, w, q, s, total[s], c, comp, nd[0]))
+            recs.append((lo, hi, st, w, me))
             log[name] = recs
+        return me
 
-    nsem = [0]
+    nsem, lastdma = [0], {}
 
-    def dma(q, out, in_, R=(), W=(), sem=None, tot=None):
+    def dma(q, out, in_, R=(), W=(), kb=512, sem=None, tot=None):
         if sem is None:
             sem = "d%d" % nsem[0]
             nsem[0] += 1
-        emit(q, lambda e: e.dma_start(out, in_), R, W, sem=sem, n=16, tot=tot or 16)
+        lastdma[q] = emit(q, lambda e: e.dma_start(out, in_), R, W, 0.06, sem=sem, n=16, tot=tot or 16, lat=2.0 + kb / 200,
+                          after=[lastdma[q]] if q in lastdma else [])
 
     def ind(win, off):
         return (win[0].indirect(off[0]), win, off)
@@ -116,51 +206,93 @@ def rank_program(g, core, T, topo):
     def rd(*vs):
         r = []
         for v in vs:
-            r += [v[1], v[2]] if len(v) == 3 else [v]
+            if isinstance(v, tuple):
+                r += [v[1], v[2]] if len(v) == 3 else [v]
         return r
 
+    def val(k):
+        return k[0] if isinstance(k, tuple) else k
+
+    def cost(a, *sides, per=None):
+        if len(a) == 3:
+            return 0.06 + cnt(a) * GAT * CY
+        if per is None:
+            per = 0.5 if all(SIZE[SCRATCH[v[1]][2]] == 2 for v in (a,) + sides) else 1
+        return max(64, cnt(a) * per) * CY
+
     def tt(out, a, b, op):
-        emit("v", lambda e: e.tensor_tensor(out[0], a[0], b[0], op), rd(a, b), [out])
+        per = 2 if len(a) != 3 and SCRATCH[a[1]][0] == S_ and SCRATCH[b[1]][0] == S_ else 1
+        emit("v", lambda e: e.tensor_tensor(out[0], a[0], b[0], op), rd(a, b), [out], cost(a, per=per))
 
     def ts(out, a, s1, op0, s2=None, op1=None):
-        R = rd(a) + ([s1] if isinstance(s1, tuple) else [])
-        k1 = s1[0] if isinstance(s1, tuple) else s1
         if op1 is None:
-            emit("v", lambda e: e.tensor_scalar(out[0], a[0], k1, None, op0), R, [out])
+            emit("v", lambda e: e.tensor_scalar(out[0], a[0], val(s1), None, op0), rd(a, s1), [out], cost(a, out))
         else:
-            emit("v", lambda e: e.tensor_scalar(out[0], a[0], k1, s2, op0, op1), R, [out])
+            emit("v", lambda e: e.tensor_scalar(out[0], a[0], val(s1), val(s2), op0, op1), rd(a, s1, s2), [out], cost(a, out))
 
     def cp(out, a):
         if len(out) == 3:
-            emit("v", lambda e: e.tensor_copy(out[0], a[0]), rd(a) + [out[2]], [out[1]])
+            emit("v", lambda e: e.tensor_copy(out[0], a[0]), [a, out[2]], [out[1]], 0.06 + cnt(a) * SCA * CY)
         else:
-            emit("v", lambda e: e.tensor_copy(out[0], a[0]), rd(a), [out])
+            emit("v", lambda e: e.tensor_copy(out[0], a[0]), rd(a), [out], cost(a, out))
 
-    def ms(out, val):
-        emit("v", lambda e: e.memset(out[0], val), [], [out])
-
-    def red(out, a):
-        emit("v", lambda e: e.tensor_reduce(out[0], a[0], AxisListType.X, OP.add), [a], [out])
+    def ms(out, v):
+        emit("v", lambda e: e.memset(out[0], v), [], [out], cost(out))
 
     def scan(out, d0, d1, init, op0, op1):
-        emit("v", lambda e: e.tensor_tensor_scan(out[0], d0[0], d1[0], init, op0, op1), [d0, d1], [out])
+        emit("v", lambda e: e.tensor_tensor_scan(out[0], d0[0], d1[0], init, op0, op1), [d0, d1], [out], cost(d0, d1, out))
 
     def act(out, a, func, bias=0.0, scale=1.0, accum=None):
-        R = rd(a) + ([bias] if isinstance(bias, tuple) else [])
-        k = bias[0] if isinstance(bias, tuple) else bias
         if accum:
-            emit("s", lambda e: e.activation(out[0], a[0], func, bias=k, scale=scale, accum_out=accum[0]), R, [out, accum])
+            emit("s", lambda e: e.activation(out[0], a[0], func, bias=val(bias), scale=scale, accum_out=accum[0]), rd(a, bias), [out, accum], cost(a, per=1) + 0.02)
         else:
-            emit("s", lambda e: e.activation(out[0], a[0], func, bias=k, scale=scale), R, [out])
+            emit("s", lambda e: e.activation(out[0], a[0], func, bias=val(bias), scale=scale), rd(a, bias), [out], cost(a, per=1))
+
+    def gather(who, out, src):
+        if who == "s":
+            act(out, src, AF.Copy)
+        else:
+            cp(out, src)
+        inturn()
+
+    turn = {}
+
+    def inturn():
+        me = len(ops) - 1
+        key = (ops[me]["q"], kind[0])
+        if key in turn:
+            ops[me]["deps"].setdefault(turn[key], False)
+        turn[key] = me
+
+    kind = [0]
 
     def mm(out, l, r, start, stop):
-        emit("p", lambda e: e.matmul(out[0], l[0], r[0], start, stop), [l, r], [out])
+        c = max(min(64, cnt(l)), cnt(r)) * (4 if SCRATCH[l[1]][2] == F else 1) * CY
+        emit("p", lambda e: e.matmul(out[0], l[0], r[0], start, stop), [l, r], [out], c)
 
-    def iota(out, pat, base, cm, flt):
-        emit("g", lambda e: e.iota(out[0], pat, base, cm, allow_small_or_imprecise_dtypes=True) if flt else e.iota(out[0], pat, base, cm), [], [out])
+    def iota(out, pat, base, cm):
+        flt = SCRATCH[out[1]][2] != I
+        emit("g", lambda e: e.iota(out[0], pat, base, cm, allow_small_or_imprecise_dtypes=True) if flt else e.iota(out[0], pat, base, cm), [], [out],
+             0.13 + 2 * cnt(out) * CY)
 
-    def asel(b, pat, op, base, cm):
-        emit("g", lambda e: e.affine_select(b[0], b[0], pat, op, 0.0, base, cm), [b], [b])
+    def asel(b, pat, op, base, cm, src=None):
+        src = src or b
+        emit("g", lambda e: e.affine_select(b[0], src[0], pat, op, 0.0, base, cm), [src], [b], 0.17 + 2 * cnt(b) * CY)
+
+    def gcopy(out, src):
+        asel(out, [[0, cnt(out)]], OP.is_ge, 1, 0, src)
+
+    def same(b, o, st):
+        asel(b, o + [[-16, 8]] + st, OP.is_ge, 0, 1)
+        asel(b, o + [[16, 8]] + st, OP.is_ge, 15, -1)
+
+    def wrap(out, src, n, m="m0p", start=True, stop=True):
+        for b in range(16):
+            mm(out, X(m, 16 - b, 144 - b), X(src, b, n, 16), start and b == 0, stop and b == 15)
+
+    def shift(b, to):
+        lo = 16 + 128 * b - (to - b)
+        return X("dg", lo, lo + 128)
 
     cores = T.cores
 
@@ -170,374 +302,359 @@ def rank_program(g, core, T, topo):
         m = sum(1 << k for k in e)
         a = topo.addr(to)
         out = T[dst][:, 0:1024]
-        emit("g", lambda q: q.remote_dma(out, src[0], T.sem["ar%d" % ix], T.sem["rl%d" % ix], a[1], a[0], m), [src], [], sem="rl%d" % ix, n=0, tot=len(e))
-        log.setdefault(dst, []).append((0, 1024, True, "x", "ar%d" % ix, len(e), {"ar%d" % ix: len(e)}, False, 0))
-        total["ar%d" % ix] = len(e)
+        me = emit("g", lambda q: q.remote_dma(out, src[0], T.sem["ar%d" % ix], T.sem["rl%d" % ix], a[1], a[0], m), [src, X("basi")], [], 0.3,
+                  sem="rl%d" % ix, n=0, tot=len(e), lat=6.0)
+        emit("x", None, [], [X(dst)], 0.0, sem="ar%d" % ix, n=0, tot=len(e), after=[me], lat=6.5)
 
-    dma("y", T.meas[:], T.mea[:], W=[X("meas")], sem="d1")
+    dma("s", T.meas[:], T.mea[:], W=[X("meas")], kb=256)
+    for c in range(4):
+        dma("y", T.bw[:, 16 * c:16 * c + 16], T.bas[15::16, 256 * c:256 * c + 256], W=[X("bw", 16 * c, 16 * c + 16)], kb=8)
+    dma("y", T.usei[:], T.use[:], W=[X("usei")], kb=768)
+    dma("y", T.dt[:, 0:1024], T.der[:], W=[X("dt", 0, 1024)], kb=1280)
+    dma("y", T.mor0[:, 0:2048], T.mor[:], W=[X("mor0", 0, 2048)], kb=1792)
+    dma("y", T.basi[:], T.bas[:], W=[X("basi")], kb=2304)
+    dma("y", T.mor1[:, 0:2048], T.mor[:], W=[X("mor1", 0, 2048)], kb=2816)
     for b in range(16):
-        dma("y" if b % 2 == 0 else "s", T.b15[b::16, 0:994], T.bas[15::16, 2 * b:2 * b + 994], W=[X("b15")] if b == 15 else [], sem="d0", tot=256)
-    nsem[0] = 2
-    dma("s", T.usei[:], T.use[:], W=[X("usei")])
-    dma("y", T.deri[:], T.der[:], W=[X("deri")])
-    dma("s", T.morw[:, MO:MD], T.mor[:], W=[X("morw", MO, MD)])
-    dma("y", T.basi[:], T.bas[:], W=[X("basi")])
-    dma("y", T.morw[:, MD:MX], T.mor[:], W=[X("morw", MD, MX)])
+        dma("y", T.b15[b::16, 0:994], T.bas[15::16, 2 * b:2 * b + 994], W=[X("b15")] if b == 15 else [], sem="d39", tot=256, kb=3300)
 
-    def same(b, o, st):
-        asel(b, o + [[-16, 8]] + st, OP.is_ge, 0, 1)
-        asel(b, o + [[16, 8]] + st, OP.is_ge, 15, -1)
-
-    ms(X("rm"), 1.0)
-    ms(X("zsp"), 0.0)
-    ms(X("rm", 0, 2048, 16), 0.0)
-    ms(X("g8"), 2048.0)
-    ms(X("id1"), 1.0)
-    ms(X("idb"), float(2 ** 23 + 1024))
-    ms(X("mvt0", 512, 640), 0.0)
-    ms(X("idh"), 1.0)
-    ms(X("idn"), -1.0)
-    ms(X("minm"), 0.0)
-    ms(X("la"), 1.0)
+    PK, P16, PEN, WZ, NM, TOT = [X("col", k, k + 1) for k in range(6)]
+    for n, v in (("rm", 1), ("zsp", 0), ("g8", 2048), ("id1", 1), ("idb", 2 ** 23), ("idh", 1), ("idn", -1), ("minm", 0), ("la1", 1), ("la2", 1), ("m8", 1),
+                 ("m8r", 1), ("b1", 1), ("tri", 1), ("ust", 1), ("one", 1), ("m0p", 0), ("m0n", 0)):
+        ms(X(n), float(v))
+    ms(X("rm", 0, 1024, 16), 0.0)
     ms(X("minm", 0, 512, 16), BIG)
-    ms(X("m8"), 1.0)
-    ms(X("b1"), 1.0)
+    ms(X("m8r", 0, 256, 8), 0.0)
+    ms(X("dg", 0, 16), 0.0)
+    ms(X("dg", 2064, 2080), 0.0)
+    for n in ("mvt0", "mvt1", "dd", "cq"):
+        ms(X(n, 512, 640), 0.0)
+    for n in ("bst0", "bst1"):
+        ms(X(n, 512, 640), -4096.0)
+    for n in ("mor0", "mor1"):
+        ms(X(n, FAR, SH), 16384.0)
+    ms(X("tl", 1024, 1032), float(FAR))
+    ms(X("cumw", 32, 40), BIG)
+    ms(NM, 0.0)
+    iota(X("pi"), [[0, 32]], 0, 1)
+    iota(X("fa"), [[256, 4], [2, 8]], 0, 0)
+    iota(X("i16"), [[16, 32]], 0, 0)
     same(X("g8"), [], [])
-    for n in ("id1", "idb", "idh", "idn"):
+    for n in ("idh", "id1", "idb", "idn"):
         asel(X(n), [[-1, 128]], OP.is_equal, 0, 1)
-    iota(X("vr0"), [[2, 512]], 0, 0, True)
-    iota(X("pi"), [[0, 32]], 0, 1, False)
-    send(X("meas"), "mq0", 0, 0)
-    asel(X("la"), [[-16, 8], [0, 8], [-1, 16]], OP.is_equal, 0, 1)
+    for k in range(16):
+        cp(X("xp", k, 2048, 16), X("idh"))
+    iota(X0("vrh"), [[256, 4], [0, 8], [16, 16]], 0, 0)
+    for par in range(2):
+        iota(X0("vrl%d" % par), [[0, 4], [2, 8], [0, 16]], par, 0)
+    for x in range(8):
+        asel(X("la1", 128 * x, 128 * x + 128), [[0, 8], [-1, 2], [-16, 8]], OP.is_equal, -2 * x, 1)
+    asel(X("la2"), [[-16, 8], [0, 8], [-1, 16]], OP.is_equal, 0, 1)
     same(X("m8"), [[0, 32]], [])
-    same(X("b1"), [], [[0, 16]])
-    iota(X("i16"), [[16, 32]], 0, 0, True)
-    iota(X("kin"), [[-1, 528]], 1024, 1, False)
+    for n in ("b1", "tri", "ust"):
+        same(X(n), [], [[0, 16]])
+    asel(X("tri"), [[1, 128]], OP.is_ge, 0, -1)
+    asel(X("ust"), [[-1, 128]], OP.is_gt, 0, 1)
+    iota(X("srow"), [[1, 128]], 0, 0)
+    ts(X("m0p", 16, 144, 16), X("g8"), 1 / 2048, OP.mult)
+    ts(X("m0n", 16, 144, 16), X("g8"), -1 / 2048, OP.mult)
+    ts(X("ia"), X("pi"), 15, OP.bitwise_and)
+    cp(PK, X("ia", 0, 1))
+    ts(X("fc", 0, 16), X("srow", 0, 16), PK, OP.is_equal)
+    for b in range(16):
+        ts(X("dg", 16 + 128 * b, 144 + 128 * b), X("idh"), X("fc", b, b + 1), OP.mult)
+    ts(P16, PK, 16.0, OP.mult)
+    ts(PEN, PK, 15.0, OP.is_lt, 8192.0, OP.mult)
+    ts(X("ib", 0, 1), X("ia", 0, 1), 1, OP.add)
+    ts(X("ic", 0, 1), X("ib", 0, 1), 3, OP.bitwise_and)
+    cp(WZ, X("ic", 0, 1))
+    ts(X("iw"), X("i16"), PK, OP.add)
+    ts(X("bj"), X("iw", 0, 8), 0.5, OP.add)
 
-    def kap(t):
-        ts(X("zt"), X("b15", t % 2, 994, 32), 97 * t, OP.add)
-        ts(X("zu"), X("zt"), 1023, OP.bitwise_and)
-        cp(X("kap%d" % t), X("zu"))
+    def kap(t, nat):
+        src = X("b15", t % 2, 994, 32) if nat else X("bw", t % 2, 64, 2)
+        ts(X("ib"), src, 97 * t, OP.add)
+        ts(X("ic"), X("ib"), 1023, OP.bitwise_and)
+        cp(KAP(t, nat), X("ic"))
 
-    def prep(t):
-        cp(X("cdf"), ind(X("usef") if t else X("usei"), X("kap%d" % t)))
-        cp(X("cdo"), X("cdf"))
-        tt(X("eq"), X("cdf"), X("vr%d" % (t % 2)), OP.is_equal)
+    def KAP(t, nat):
+        return X("kap", 64 * t + 32 * nat, 64 * t + 32 * nat + 32)
 
-    late = []
+    def flags(par, der, bank):
+        mm(X(bank), X("idh"), X("bsh%d" % par), True, True)
+        tt(X("neq"), X(bank), der, OP.not_equal)
+        mm(X(bank), X("tri"), X("neq"), True, True)
+        act(X(bank), X(bank), AF.Relu, bias=PEN, scale=-8192.0)
+        tt(X("tl", par, 1024, 2), der, X(bank), OP.subtract)
 
-    def sub_abs(name, lo, rep, rlo):
+    def search(t):
+        par = t % 2
+        kind[0] = "search"
         for h in range(2):
-            a = X(name, lo + 512 * h, lo + 512 * h + 512)
-            mm(X("pX%d" % h), X("idh"), a, True, False)
-            mm(X("pX%d" % h), X("idn"), X(rep, rlo + 512 * h, rlo + 512 * h + 512), False, True)
-        for h in range(2):
-            act(X(name, lo + 512 * h, lo + 512 * h + 512), X("pX%d" % h), AF.Abs)
-
-    def chunk(t, c):
-        sl = X("dm", 1024 * c, 1024 * c + 1024)
-        rep = "rep%d" % (t % 2)
-        src = ind(X("meas"), X("cdo", 64 * c, 64 * c + 64))
-        if MSPLIT[t][c] == "v":
-            tt(sl, src, X(rep, 1024 * c, 1024 * c + 1024), OP.subtract)
-            act(sl, sl, AF.Abs)
-        else:
-            act(sl, src, AF.Copy)
-            sub_abs("dm", 1024 * c, rep, 1024 * c)
-        if c % 2:
-            late.append(c // 2)
-
-    def flush():
-        while late:
-            j = late.pop(0)
-            blk = X("pK", 128 * j, 128 * j + 128)
-            mm(blk, X("cdf", 128 * j, 128 * j + 128), X("id1"), True, False)
-            mm(blk, X("eq", 128 * j, 128 * j + 128), X("idb"), False, False)
-            for k in range(16):
-                mm(X("pK", 128 * j + k, 128 * j + 128, 16), X("dm", 2048 * j + k, 2048 * j + 2048, 16), X("g8"), False, k == 15)
-
-    done = {0: 0, 1: 0, 2: 0, 3: 8}
-
-    def fill(t, n):
-        for _ in range(n):
-            flush()
-            if done[t] < 8:
-                chunk(t, done[t])
-                done[t] += 1
-
-    def lists(c, offs, who, base, n):
-        src = ind(X("morw", MO, 4624) if base else X("morw", MO, MD), X(offs, n * c // 16, n * c // 16 + n // 16))
-        out = X("gd", n * c, n * c + n)
-        if who == "s":
-            act(out, src, AF.Copy)
-        else:
-            cp(out, src)
+            act(X("cdf", 256 * h, 256 * h + 256), ind(X("usei"), X("kap", 64 * t + 16 * h, 64 * t + 16 * h + 16)), AF.Copy)
+            cp(X("cdo", 256 * h, 256 * h + 256), X("cdf", 256 * h, 256 * h + 256))
+        mm(X("pB"), X0("one"), X0("vrh"), True, False)
+        mm(X("pB"), X0("one"), X0("vrl%d" % par), False, True)
+        tt(X("eq"), X("pB"), X("cdf"), OP.is_equal)
+        for c in range(16):
+            sl = X("dm", 512 * c, 512 * c + 512)
+            src = ind(X("meas"), X("cdo", 32 * c, 32 * c + 32))
+            how = SEARCH[t][c]
+            if how == "v":
+                tt(sl, src, X("rep%d" % par, 512 * c, 512 * c + 512), OP.subtract)
+                inturn()
+                act(sl, sl, AF.Abs)
+            else:
+                bank = X("pF" if t or c % 2 else "pU")
+                j = c // 4
+                gather(how, sl, src)
+                mm(bank, X("mpt%d" % par, 128 * j, 128 * j + 128), X("xp", 512 * (c % 4), 512 * (c % 4) + 512), True, False)
+                mm(bank, X("idh"), sl, False, True)
+                act(sl, bank, AF.Abs)
+        for j in KEYS[t]:
+            if True:
+                blk = X("pK", 128 * j, 128 * j + 128)
+                mm(blk, X("cdf", 128 * j, 128 * j + 128), X("id1"), True, False)
+                mm(blk, X("eq", 128 * j, 128 * j + 128), X("idb"), False, False)
+                for k in range(16):
+                    mm(X("pK", 128 * j + k, 128 * j + 128, 16), X("dm", 2048 * j + k, 2048 * j + 2048, 16), X("g8"), False, k == 15)
+        scan(X("ks"), X("minm"), X("pK"), BIG, OP.max, OP.min)
+        ts(X("ia"), X("ks", 15, 512, 16), float(2 ** 23 - 1024), OP.min)
+        ts(X("ib"), X("ia"), 2047, OP.bitwise_and)
+        cp(X("mh"), X("ib"))
+        for x in range(8):
+            mm(X("pF", 32 * x, 32 * x + 32), X("la1", 128 * x, 128 * x + 128), X("mh"), True, True)
+        tt(X("um"), X("pF", 0, 256), X("m8"), OP.mult)
+        scan(X("us"), X("m8r"), X("um"), 0.0, OP.mult, OP.add)
+        for c in range(4):
+            cp(X("wf", 8 * c, 8 * c + 8), X("us", 8 * c + 7, 256, 32))
+        cp(X("wo"), X("wf"))
+        cp(X("ia"), X("wf"))
+        ts(X("ib"), X("ia"), 1, OP.bitwise_and)
+        ts(X("fa"), X("ib"), -2.0, OP.mult, 1.0, OP.add)
+        tt(X("fb"), X("fa"), X("wf"), OP.add)
+        tt(X("dw"), X("fb"), X("old", 32 * t, 32 * t + 32), OP.subtract)
 
     flip = [0]
 
-    def wide(c, dist, mv, n=1024):
-        lo = (c % (2048 // n)) * n
-        w = n // 16
-        scan(X("es", lo, lo + n), X("rm", 0, n), X("gd", n * c, n * c + n), 0.0, OP.mult, OP.max)
-        flip[0] ^= 1
-        px = X("pX%d" % flip[0], 0, w)
-        mm(px, X("idh"), X("es", lo + 15, lo + n, 16), True, False)
-        mm(px, X("idn"), X(mv, w * c, w * c + w), False, True)
-        act(X(dist, w * c, w * c + w), px, AF.Abs)
+    def lists(who, mor, offs, dist, mv, n, ends):
+        lo = 0
+        kind[0] = "lists"
+        for c, w in enumerate(who):
+            k = n // 16
+            a = X("gd", n * c, n * c + n)
+            gather(w, a, ind(X(mor, 0, SH), X(offs, k * c, k * c + k)))
+            e = (n * c) % 4096
+            scan(X("es", e, e + n), X("rm", 0, n), a, 0.0, OP.mult, OP.max)
+            px = "pX%d" % flip[0]
+            mm(X(px, k * c, k * c + k), X("idn"), X(mv, k * c, k * c + k), True, False)
+            mm(X(px, k * c, k * c + k), X("idh"), X("es", e + 15, e + n, 16), False, True)
+            if c in ends:
+                act(X(dist, lo, k * c + k), X(px, lo, k * c + k), AF.Abs)
+                lo = k * c + k
+                flip[0] ^= 1
 
-    def tl_a(par):
-        tt(X("neq"), X("dri%d" % par, 0, 512), X("basi", par, 1024, 2), OP.not_equal)
-        mm(X("pC"), X("tri"), X("neq"), True, True)
-        act(X("sg"), X("pC"), AF.Sign, bias=X("thr"))
-        act(X("pC"), X("sg"), AF.Copy, bias=2048.0, scale=2048.0)
-
-    def tl_b(par):
-        tt(X("tl", par, 1024, 2), X("pC"), X("dri%d" % par, 0, 512), OP.add)
-
-    def z_tab(par):
-        mm(X("pM"), X("wz"), X("mvt%d" % par, 0, 512), True, True)
-        cp(X("kin", 0, 512), X("pM"))
-        ts(X("kin", 0, 512), X("kin", 0, 512), 3, OP.bitwise_and)
-        cp(X("junk"), X("kin", 0, 512))
+    send(X("meas"), "mq0", 0, 0)
+    kap(0, 0)
+    for par in range(2):
+        mvp = "mvp%d" % par
+        ts(X("po%d" % par), X("fa"), P16, OP.add, float(par), OP.add)
+        act(X(mvp), ind(X("meas"), X("po%d" % par)), AF.Copy)
+        for j in range(4):
+            mm(X("pX%d" % par, 128 * j, 128 * j + 128), X(mvp, 128 * j, 128 * j + 128), X("idn"), True, True)
+        act(X("mpt%d" % par), X("pX%d" % par), AF.Copy)
+        lo = 2048 if par == 0 else 0
+        for c in range(lo // 1024):
+            cp(X("zsp", 0, 1024, 16), X(mvp, 64 * c, 64 * c + 64))
+            scan(X("rep0", 1024 * c, 1024 * c + 1024), X("rm"), X("zsp"), 0.0, OP.mult, OP.add)
+        for k in range(16):
+            gcopy(X("rep%d" % par, lo + k, REP, 16), X(mvp, lo // 16, REP // 16))
+        cp(X("mvt%d" % par, 0, 512), X("meas", par, 1024, 2))
+        cp(X("dro%d" % par), X("dt", par, 1024, 2))
+        gcopy(X("bsh%d" % par), X("basi", par, 1024, 2))
+        ts(X("bst%d" % par, 0, 512), X("basi", par, 1024, 2), -4096.0, OP.add)
+    send(X("usei"), "uq0", 0, 1)
+    cp(X("u16"), X("usei", 0, 592))
+    for t in range(3):
         for b in range(16):
-            mm(X("pU", 256, 288), X("dg", 128 * b, 128 * b + 128), X("junk", b, 512, 16), b == 0, b == 15)
-        cp(X("zw%d" % par), X("pU", 256, 288))
-
-    cp(X("mvt0", 0, 512), X("meas", 0, 1024, 2))
-    for k in range(16):
-        act(X("rep0", 4096 + k, 8192, 16), X("mvt0", 256, 512), AF.Copy)
-    for c in range(2):
-        cp(X("zsp", 0, 2048, 16), X("mvt0", 128 * c, 128 * c + 128))
-        scan(X("rep0", 2048 * c, 2048 * c + 2048), X("rm"), X("zsp"), 0.0, OP.mult, OP.add)
-    kap(0)
-    prep(0)
-    fill(0, 1)
-    cp(X("dri0", 0, 512), X("deri", 0, 1024, 2))
-    cp(X("dro0"), X("dri0", 0, 512))
-    fill(0, 1)
-    ms(X("bm"), -1.0)
-    ms(X("one"), 1.0)
-    ms(X("tri"), 1.0)
-    ms(X("dri0", 512, 640), 0)
-    ms(X("dri1", 512, 640), 0)
-    ms(X("nd", 512, 640), 0)
-    ms(X("mvt1", 512, 640), 0.0)
-    cp(X("mvt1", 0, 512), X("meas", 1, 1024, 2))
-    same(X("bm"), [], [[0, 16]])
-    iota(X("tl", 1024, 2048), [[0, 1024]], 6144, 0, True)
-    same(X("tri"), [], [[0, 16]])
-    asel(X("tri"), [[1, 128]], OP.is_ge, 0, -1)
-    for k in range(16):
-        emit("g", lambda e: e.affine_select(T.rep1[:, k:8192:16], T.mvt1[:, 0:512], [[0, 512]], OP.is_ge, 0.0, 1, 0), [X("mvt1", 0, 512)],
-             [X("rep1")] if k == 15 else [])
-
-    def setup_0():
-        ts(X("pk"), X("pi"), 15, OP.bitwise_and)
-        ts(X("thr"), X("pk", 0, 1), 15, OP.is_ge, 1.5, OP.mult)
-        ts(X("thr"), X("thr"), -0.5, OP.add)
-        tl_a(0)
-        cp(X("dri1", 0, 512), X("deri", 1, 1024, 2))
-        ms(X("m8r"), 1.0)
-        ms(X("m8r", 0, 256, 8), 0.0)
-
-    def setup_1():
-        cp(X("usef"), X("usei"))
-        send(X("usef"), "uq0", 0, 1)
-        tl_b(0)
-        tl_a(1)
-
-    def setup_a():
-        for par in range(2):
-            ts(X("bst%d" % par, 0, 512), X("basi", par, 1024, 2), 2048.0, OP.add)
-            ms(X("bst%d" % par, 512, 640), 2048.0)
-        ms(X("morw", MX, 4624), 16384.0)
-        ms(X("marg"), 0.0)
-        ms(X("on"), 1.0)
-        tl_b(1)
-        tt(X("iw"), X("pk"), X("i16"), OP.add)
-        ts(X("bj"), X("iw", 0, 8), 0.5, OP.add)
-        ts(X("j2"), X("iw", 0, 8), 2.0, OP.mult)
-        send(X("tl", 0, 1024), "tq0", 0, 2)
-        iota(X("xr"), [[2, 1024], [-1, 2]], 1, 0, True)
-        iota(X("vr1"), [[2, 512]], 1, 0, True)
-        iota(X("dg"), [[0, 2048]], 1, 0, True)
-        asel(X("dg"), [[0, 16], [-16, 8], [-1, 16]], OP.is_equal, 0, 1)
-        asel(X("dg"), [[-1, 16], [0, 8], [1, 16]], OP.is_equal, 0, 0)
-        send(X("meas"), "mq1", 1, 3)
-        send(X("meas"), "mq2", 2, 6)
-
-    def setup_b():
-        ms(X("gds", 512, 640), -100000.0)
-        ms(X("got", 512, 640), 0.0)
-        ms(X("cq", 512, 640), 0.0)
-        ts(X("kin"), X("kin"), 15, OP.bitwise_and)
-        ts(X("km"), X("kin"), 0, OP.is_equal)
-        kap(1)
-        kap(2)
-
-    def setup_c():
-        cp(X("dro1"), X("dri1", 0, 512))
-        ts(X("jp"), X("pk", 0, 1), 1.0, OP.add)
-        ts(X("wz"), X("b1"), X("jp"), OP.mult)
-        z_tab(0)
-        z_tab(1)
+            mm(X("pS", 32 * t, 32 * t + 32), shift((b + t) % 16, b), X("u16", 37 * t + b, 37 * t + 512, 16), b == 0, b == 15)
+    cp(X("old"), X("pS", 0, 96))
+    for par in range(2):
+        flags(par, X("dt", par, 1024, 2), ("pB", "pG")[par])
+        ts(X("zs"), X("mvt%d" % par, 0, 512), WZ, OP.mult)
+        wrap(X("pS", 96 + 32 * par, 128 + 32 * par), "zs", 512)
+    cp(X("zw"), X("pS", 96, 160))
+    send(X("tl", 0, 1024), "tq0", 0, 2)
+    for t in range(3):
+        w = (32 * t, 32 * t + 32)
+        if t:
+            kap(t, 0)
+        kap(t, 1)
+        ts(X("ia"), X("zw", 32 * (t % 2), 32 * (t % 2) + 32), float(t), OP.add)
+        ts(X("ib"), X("ia"), 3, OP.bitwise_and)
+        ts(X("fb"), X("iw"), 4.0, OP.mult)
+        tt(X("tgt", *w), X("fb"), X("ib"), OP.add)
+        ts(X("epos", *w), X("iw"), float(E0 if t < 2 else 0), OP.add)
+        ts(X("dpos", *w), X("iw"), 1.0 if t < 2 else 0.0, OP.mult, float(t - E0 if t < 2 else 512), OP.add)
+    send(X("meas"), "mq1", 1, 3)
+    send(X("meas"), "mq2", 2, 6)
+    search(0)
 
     for t in range(3):
         par = t % 2
-        mvt, bst, dri = "mvt%d" % par, "bst%d" % par, "dri%d" % par
-        for c in range(4):
-            lists(c, "dro%d" % par, DSPLIT[t][c], 0, 2048)
-            if t and c == 0:
-                tl_a(1 - par)
-            fill(t, DFILL[t][c] if c < 3 else 8)
-            if t == 0 and c < 3:
-                (setup_0, setup_1, setup_a)[c]()
-            if t and c == 1:
-                tl_b(1 - par)
-                send(X("tl", 0, 1024), "tq%d" % t, t, 5 if t == 1 else 8)
-            if 1 <= c < 3:
-                wide(c - 1, "dd", mvt, 2048)
-        flush()
-        scan(X("ks"), X("minm"), X("pK"), BIG, OP.max, OP.min)
-        for a in range(8):
-            mm(X("pU", 32 * a, 32 * a + 32), X("la", 128 * a, 128 * a + 128), X("ks", 15, 512, 16), True, True)
-        wide(2, "dd", mvt, 2048)
-        tt(X("um"), X("pU", 0, 256), X("m8"), OP.mult)
-        wide(3, "dd", mvt, 2048)
-        mm(X("pD"), X("b1"), X("dd"), True, True)
-        mm(X("pG"), X("bm"), X("dd"), True, False)
-        scan(X("us"), X("m8r"), X("um"), 0.0, OP.mult, OP.add)
-        mine = [c for c in range(8) if "G%d" % c not in EORD[t]]
-        ahead = []
-
-        def gather_e(n, top):
-            for c in [c for c in mine if c not in ahead and c < top][:n]:
-                lists(c, "eo", "s", 1, 1024)
-                ahead.append(c)
-
+        mvt, bst, mor, nxt = "mvt%d" % par, "bst%d" % par, "mor%d" % par, "mor%d" % (1 - par)
+        w = (32 * t, 32 * t + 32)
+        if t:
+            dma("y", T[nxt][:, 0:2048], T[mor][:, 0:2048], R=[X(mor, 0, 2048)], W=[X(nxt, 0, 2048)])
+        lists(DWHO[t], mor, "dro%d" % par, "dd", mvt, 1024, (3, 7))
+        wrap(X("pG", 0, 32), "dd", 512, "m0n", True, False)
         for h in range(2):
-            for j in (2 * h, 2 * h + 1):
-                cp(X("wi", 8 * j, 8 * j + 8), X("us", 8 * j + 7, 256, 32))
-            w = (16 * h, 16 * h + 16)
-            ts(X("wj", *w), X("wi", *w), 2047, OP.bitwise_and)
-            cp(X("wo", *w), X("wj", *w))
             l = (256 * h, 256 * h + 256)
-            tt(X("ec", *l), ind(X("tl"), X("wo", *w)), X(bst, *l), OP.max)
-            ts(X("eo", *l), X("ec", *l), -2048.0, OP.add)
-            if h == 0:
-                gather_e(4, 4)
-        if t == 0:
-            setup_b()
-        us = X("usef", 37 * t, 37 * t + 512)
-        gather_e(4 - len(ahead), 8)
-        for tok in EORD[t].split():
-            c = int(tok[1])
-            if tok[0] == "G":
-                lists(c, "eo", "v", 1, 1024)
-                continue
-            gather_e(1, 8)
-            wide(c, "ee", mvt)
-            if c == 2:
-                cp(X("dk"), ind(X("xr"), X("wo")))
-            if c == 4:
-                tt(X("pM"), X("dk"), us, OP.subtract)
-                tt(X("dk"), X("pM"), X("km", t, t + 512), OP.mult)
-        mm(X("pG"), X("b1"), X("ee"), False, True)
-        ts(X("fail"), X("pG"), X("marg"), OP.add, 0.0, OP.is_ge)
-        scan(X("cum"), X("fail"), X("fail"), 0.0, OP.add, OP.max)
-        for a in range(8 - CNTV[t]):
-            act(X("junk"), X("cum"), AF.Sign, bias=X("bj", a, a + 1), scale=-1.0, accum=X("acc", a, a + 1))
-        act(X("cq", 0, 512), ind(X("uq%d" % t), X("kap%d" % t)), AF.Copy)
-        act(X("gds", 0, 512), X("pD"), AF.Copy)
-        act(X("got", 0, 512), X("fail"), AF.Copy, bias=1.0, scale=-1.0)
-        mm(X("pC"), X("idn"), X("fail"), True, False)
-        mm(X("pC"), X("idh"), X("one"), False, True)
-        tt(X("pM"), X("dk"), X("pC"), OP.mult)
-        tt(us, X("pM"), us, OP.add)
+            tt(X("ec", *l), ind(X("tl"), X("wo", 16 * h, 16 * h + 16)), X(bst, *l), OP.max)
+            ts(X("dt", E0 + l[0], E0 + l[1]), X("ec", *l), 4095, OP.bitwise_and)
+            cp(X("eo", *l), X("dt", E0 + l[0], E0 + l[1]))
+        lists(EWHO[t], mor, "eo", "ee", mvt, 1024, (3, 6, 7))
+        wrap(X("pG", 0, 32), "ee", 512, "m0p", False, True)
+        ts(X("fw", 0, 32), X("pG", 0, 32), NM, OP.is_ge)
+        ts(X("gw"), X("pG", 0, 32), NM, OP.is_lt)
+        mm(X("pS", 0, 32), X("b1"), X("fw", 0, 32), True, True)
+        mm(X("pS", 32, 64), X("ust"), X("fw", 0, 32), True, True)
+        scan(X("bc"), X("one", 0, 32), X("pS", 0, 32), 0.0, OP.mult, OP.add)
+        tt(X("cumw", 0, 32), X("bc"), X("pS", 32, 64), OP.subtract)
+        for a in range(8):
+            act(X("junk", 32 * a, 32 * a + 32), X("bc"), AF.Sign, bias=X("bj", a, a + 1), scale=-1.0, accum=X("acc", a, a + 1))
+        ts(X("blk"), X("acc"), 0.5, OP.mult, 16.0, OP.add)
+        tt(X("cmp"), ind(X("cumw"), X("blk")), X("srow"), OP.is_le)
+        wrap(X("pS", 64, 72), "cmp", 128)
+        ts(X("ga"), X("acc"), 32.0, OP.is_ge)
+        tt(X("ga"), X("ga"), X("iw", 0, 8), OP.mult)
+        ts(X("gb"), X("acc"), 8.0, OP.mult, 256.0, OP.add)
+        tt(X("ga"), X("ga"), X("gb"), OP.add)
+        tt(X("sf"), X("pS", 64, 72), X("ga"), OP.add)
+        cp(X("sel"), X("sf"))
+        tt(X("vw"), X("dw"), X("gw"), OP.mult)
+        for b in range(16):
+            mm(X("pB", b, 512, 16), shift(b, (b + t) % 16), X("vw"), True, True)
+        us = X("usei", 37 * t, 37 * t + 512)
+        act(X("cq", 0, 512), ind(X("uq%d" % t), KAP(t, 1)), AF.Copy)
+        tt(us, X("pB"), us, OP.add)
         if t < 2:
-            send(X("usef"), "uq%d" % (t + 1), t + 1, 4 if t == 0 else 7)
-            prep(t + 1)
+            send(X("usei"), "uq%d" % (t + 1), t + 1, 4 if t == 0 else 7)
         else:
+            gcopy(X("usef"), X("usei"))
             dma("y", T.yu[:], T.usef[:], R=[X("usef")])
-        tt(X("pM"), X("ec"), X("pC"), OP.mult)
-        tt(X("nd", 0, 512), X("pM"), X(dri, 0, 512), OP.max)
-        for a in range(8 - CNTV[t], 8):
-            ts(X("neq"), X("cum"), X("bj", a, a + 1), OP.is_le)
-            red(X("acc", a, a + 1), X("neq"))
-            ts(X("acc", a, a + 1), X("acc", a, a + 1), 2.0, OP.mult, -512.0, OP.add)
-        if t == 0:
-            setup_c()
-        fill(t + 1, FILL[t][0])
-        ts(X("sm"), X("acc"), 511.0, OP.is_gt)
-        tt(X("sm"), X("sm"), X("j2"), OP.mult)
-        tt(X("sm"), X("sm"), X("acc"), OP.add)
-        ts(X("sel"), X("sm"), 0.5, OP.mult, 256.0, OP.add)
+        new = X("dt", D0, D0 + 512) if t == 0 else X("ydb", par, 1024, 2)
+        tt(X("fa"), X("fw", 0, 32), X("dpos", *w), OP.mult)
+        tt(X("fb"), X("fa"), X("epos", *w), OP.add)
+        cp(X("ua"), X("fb"))
+        cp(new, ind(X("dt", 0, D0) if t < 2 else X("dt", E0, D0 + 512), X("ua")))
+        ts(X("fc"), X("fw", 0, 32), float(SH), OP.mult)
+        tt(X("fc"), X("fc"), X("tgt", *w), OP.add)
+        cp(X("ub"), X("fc"))
+        for h in range(4):
+            cp(ind(X(nxt), X("ub", 8 * h, 8 * h + 8)), X(mvt, 128 * h, 128 * h + 128))
         cp(X("c2f"), ind(X("cq"), X("sel")))
         cp(X("c2o"), X("c2f"))
-        cp(X("mv2"), ind(X(mvt), X("sel")))
-        cp(X("zsp", 0, 2048, 16), X("mv2"))
-        scan(X("rp2"), X("rm"), X("zsp"), 0.0, OP.mult, OP.add)
-        mm(X("pC", 0, 128), X("c2f"), X("id1"), True, False)
-        act(X("gd", 5120, 6144), ind(X("mq%d" % t), X("c2o", 64, 128)), AF.Copy)
-        tt(X("gd", 4096, 5120), ind(X("mq%d" % t), X("c2o", 0, 64)), X("rp2", 0, 1024), OP.subtract)
-        sub_abs("gd", 5120, "rp2", 1024)
-        act(X("gd", 4096, 5120), X("gd", 4096, 5120), AF.Abs)
-        for k in range(16):
-            mm(X("pC", k, 128, 16), X("gd", 4096 + k, 6144, 16), X("g8"), False, k == 15)
-        act(X("gd2"), ind(X("gds"), X("sel")), AF.Copy)
-        cp(X("bs2"), ind(X(bst), X("sel")))
-        cp(X("dr2"), ind(X(dri), X("sel")))
-        fill(t + 1, FILL[t][1])
-        scan(X("ks2"), X("minm", 0, 128), X("pC", 0, 128), BIG, OP.max, OP.min)
-        for a in range(8):
-            mm(X("pU", 8 * a, 8 * a + 8), X("la", 128 * a, 128 * a + 128), X("ks2", 15, 128, 16), True, True)
-        fill(t + 1, FILL[t][2])
-        tt(X("um2"), X("pU", 0, 64), X("m8", 0, 64), OP.mult)
-        scan(X("us2"), X("m8r", 0, 64), X("um2"), 0.0, OP.mult, OP.add)
-        cp(X("wi", 0, 8), X("us2", 7, 64, 8))
-        ts(X("wj", 0, 8), X("wi", 0, 8), 2047, OP.bitwise_and)
-        cp(X("w2o"), X("wj", 0, 8))
+        act(X("mv2"), ind(X(mvt), X("sel")), AF.Copy)
+        mm(X("pS", 128, 256), X("mv2"), X("idn"), True, True)
+        act(X("mt2"), X("pS", 128, 256), AF.Copy)
+        mm(X("pU", 0, 128), X("c2f"), X("id1"), True, False)
+        kind[0] = "lists"
+        for q in range(4):
+            a = X("g2", 512 * q, 512 * q + 512)
+            px = X("pX%d" % (q % 2))
+            src = ind(X("mq%d" % t), X("c2o", 32 * q, 32 * q + 32))
+            if ASK[q] == "v":
+                rp = X("es", 2048 + 512 * q, 2560 + 512 * q)
+                z = 512 * (q % 2)
+                cp(X("zsp", z, z + 512, 16), X("mv2", 32 * q, 32 * q + 32))
+                scan(rp, X("rm", 0, 512), X("zsp", z, z + 512), 0.0, OP.mult, OP.add)
+                tt(a, src, rp, OP.subtract)
+                inturn()
+                act(a, a, AF.Abs)
+            else:
+                gather(ASK[q], a, src)
+                mm(px, X("mt2"), X("xp", 512 * q, 512 * q + 512), True, False)
+                mm(px, X("idh"), a, False, True)
+                act(a, px, AF.Abs)
+            for k in range(16):
+                o = X("pU", k, 128, 16)
+                mm((T.pU[32 * q:32 * q + 32, k:128:16],) + o[1:], X("g2", 512 * q + k, 512 * q + 512, 16), X("g8"), False, k == 15)
+        act(X("dd2"), ind(X("dd"), X("sel")), AF.Copy)
+        act(X("bs2"), ind(X(bst), X("sel")), AF.Copy)
+        wrap(X("pG", 32, 40), "dd2", 128, "m0n", True, False)
+        ts(X("zs2"), X("mv2"), WZ, OP.mult)
+        wrap(X("pS", 72, 80), "zs2", 128)
+        ts(X("ja"), X("pS", 72, 80), float(t), OP.add)
+        ts(X("jb"), X("ja"), 3, OP.bitwise_and)
+        ts(X("ga"), X("sf"), 4.0, OP.mult)
+        tt(X("tg2"), X("ga"), X("jb"), OP.add)
+        ts(X("pd2"), X("sf"), 2.0 if t else 1.0, OP.mult, float(par), OP.add)
+        scan(X("ks", 0, 128), X("minm", 0, 128), X("pU", 0, 128), BIG, OP.max, OP.min)
+        cp(X("ja"), X("ks", 15, 128, 16))
+        ts(X("jc"), X("ja"), 2047, OP.bitwise_and)
+        cp(X("mh", 0, 8), X("jc"))
+        for x in range(8):
+            mm(X("pU", 256 + 8 * x, 264 + 8 * x), X("la2", 128 * x, 128 * x + 128), X("mh", 0, 8), True, True)
+        tt(X("um", 0, 64), X("pU", 256, 320), X("m8", 0, 64), OP.mult)
+        scan(X("us", 0, 64), X("m8r", 0, 64), X("um", 0, 64), 0.0, OP.mult, OP.add)
+        cp(X("w2o"), X("us", 7, 64, 8))
         tt(X("ec2"), ind(X("tq%d" % t), X("w2o")), X("bs2"), OP.max)
-        ts(X("eo2"), X("ec2"), -2048.0, OP.add)
-        lists(0, "eo2", "s", 1, 1024)
-        lists(1, "eo2", "v", 1, 1024)
-        wide(0, "ee2", "mv2")
-        wide(1, "ee2", "mv2")
-        mm(X("pD", 0, 128), X("b1"), X("ee2"), True, True)
-        cp(X("zi"), X("zw%d" % par))
-        ts(X("zt"), X("zi"), t, OP.add)
-        ts(X("zu"), X("zt"), 3, OP.bitwise_and)
-        ts(X("zc"), X("iw"), 3.0, OP.mult, float(MO), OP.add)
-        tt(X("zc"), X("zc"), X("zu"), OP.add)
-        fill(t + 1, FILL[t][3])
-        tt(X("x2"), X("pD", 0, 128), X("gd2"), OP.subtract)
-        ts(X("ad2"), X("x2"), X("marg"), OP.add, 0.0, OP.is_lt)
-        cp(ind(X("got"), X("sel")), X("ad2"))
-        for b in range(16):
-            mm(X("pU", 256, 288), X("dg", 128 * b, 128 * b + 128), X("got", b, 512, 16), b == 0, b == 15)
-        tt(X("y2"), X("ad2"), X("ec2"), OP.mult)
-        tt(X("n2"), X("y2"), X("dr2"), OP.max)
-        tt(X("gf"), X("pU", 256, 288), X("zc"), OP.mult)
-        tt(X("gf"), X("gf"), X("iw"), OP.add)
-        cp(X("gu"), X("gf"))
-        cp(ind(X("morw", 0, MD), X("gu")), X(mvt, 0, 512))
+        ts(X("ea2"), X("ec2"), 4095, OP.bitwise_and)
+        cp(X("eo2"), X("ea2"))
+        lists("svsv", mor, "eo2", "ee2", "mv2", 512, (3,))
+        wrap(X("pG", 32, 40), "ee2", 128, "m0p", False, True)
+        ts(X("f2m"), X("pG", 32, 40), NM, OP.is_ge, float(SH), OP.mult)
+        ts(X("f2d"), X("pG", 32, 40), NM, OP.is_ge, 1280.0 if t else 640.0, OP.mult)
+        ts(X("fw", 32, 40), X("pG", 32, 40), NM, OP.is_ge)
+        tt(X("ga"), X("f2m"), X("tg2"), OP.add)
+        cp(X("uc"), X("ga"))
+        cp(ind(X(nxt), X("uc")), X("mv2"))
+        tt(X("gb"), X("f2d"), X("pd2"), OP.add)
+        cp(X("ud"), X("gb"))
+        cp(ind(X("ydb") if t else X("dt", D0, 2816), X("ud")), X("ea2"))
         if t < 2:
-            red(X("cn"), X("pU", 256, 288))
-            mm(X("pC", 0, 1), X("on"), X("cn"), True, True)
-            dma("y", T.morw[:, MD:MX], T.morw[:, MO:MD], R=[X("morw", MO, MD)], W=[X("morw", MD, MX)])
-        else:
-            dma("s", T.ym[:], T.morw[:, MO:MD], R=[X("morw", MO, MD)])
-        cp(ind(X("nd"), X("sel")), X("n2"))
-        ts(X(dri), X("nd"), 2047, OP.bitwise_and)
-        if t < 2:
-            cp(X("wi", 0, 1), X("pC", 0, 1))
-            ts(X("wj", 0, 1), X("wi", 0, 1), 127, OP.bitwise_and)
-            cp(X("marg"), X("wj", 0, 1))
-            if t == 0:
-                cp(X("dro0"), X("dri0", 0, 512))
-        if t > 0:
-            cp(X("ydb", par, 1024, 2), X(dri, 0, 512))
-    dma("y", T.yd[:], T.ydb[:], R=[X("ydb")])
+            search(t + 1)
+            flags(par, new, "pB")
+            send(X("tl", 0, 1024), "tq%d" % (t + 1), t + 1, 5 if t == 0 else 8)
+            mm(X("pS", 80, 120), X("one"), X("fw"), True, True)
+            emit("v", lambda e: e.tensor_reduce(TOT[0], T.pS[:, 80:120], AxisListType.X, OP.add), [X("pS", 80, 120)], [TOT], 64 * CY)
+            ts(X("ja", 0, 1), TOT, -1.0, OP.mult)
+            ts(X("jb", 0, 1), X("ja", 0, 1), 127, OP.bitwise_and)
+            ts(NM, X("jb", 0, 1), -1.0, OP.mult)
+        if t == 0:
+            cp(X("dro0"), new)
+    dma("s", T.ym[:], T.mor1[:, 0:2048], R=[X("mor1", 0, 2048)])
+    dma("y", T.yd[:], T.ydb[:, 0:1024], R=[X("ydb", 0, 1024)])
+
+    if not ORDER:
+        ORDER.extend(arrange(ops))
+    order = ORDER
+
+    queue = {"v": g.vector, "s": g.scalar, "p": g.tensor, "g": g, "y": g.sync}
+    clock = {q: {} for q in queue}
+    total = {}
+    for pos, i in enumerate(order):
+        o = ops[i]
+        q = o["q"]
+        o["pos"] = pos
+        if q == "x":
+            total[o["sem"]] = o["tot"]
+            o["at"], o["known"] = (o["sem"], o["tot"]), {o["sem"]: o["tot"]}
+            continue
+        for d in sorted((d for d, wait in o["deps"].items() if wait), key=lambda d: -ops[d]["pos"]):
+            s, c = ops[d]["at"]
+            if clock[q].get(s, 0) < c:
+                queue[q].wait_ge(T.sem[s], c)
+                for s2, c2 in ops[d]["known"].items():
+                    clock[q][s2] = max(clock[q].get(s2, 0), c2)
+        s = "c" + q if o["comp"] else o["sem"]
+        ins = o["fn"](queue[q])
+        if o["n"]:
+            ins.then_inc(T.sem[s], o["n"])
+        total[s] = total.get(s, 0) + 1 if o["comp"] else o["tot"]
+        o["at"] = (s, total[s])
+        o["known"] = dict(clock[q])
+        o["known"][s] = total[s]
     for s in sorted(total):
         if clock["g"].get(s, 0) < total[s]:
             g.wait_ge(T.sem[s], total[s])

@@ -1,4 +1,4 @@
-from concourse.mybir import AluOpType as OP, AxisListType, ActivationFunctionType as AF
+from concourse.mybir import AluOpType as OP, ActivationFunctionType as AF
 
 S_, P_ = "sbuf", "psum"
 F, B, H, I, U = "float32", "bfloat16", "float16", "int32", "uint16"
@@ -26,17 +26,16 @@ _buf("basi usei uq0 uq1 uq2", 1024, I)
 _buf("dt", 2816, I)
 _buf("meas mq0 mq1 mq2 rm zsp la1 la2", 1024, B)
 _buf("mor0 mor1", 4624, B)
-_buf("usef tq0 tq1 tq2", 1024, F)
+_buf("tq0 tq1 tq2", 1024, F)
 _buf("tl", 1032, F)
 _buf("ydb", 2560, F)
 _buf("mvt0 mvt1 dd", 640, B)
-_buf("mvp0 mvp1 mpt0 mpt1 eq ee neq minm vrh vrl0 vrl1 oner", 512, B)
+_buf("mvp0 mvp1 mpt0 mpt1 eq ee neq minm vrh vrl0 vrl1", 512, B)
 _buf("bst0 bst1 cq", 640, F)
 _buf("dro0 dro1 cdo eo", 512, U)
-_buf("rep0 rep1", 6144, B)
-_buf("es", 4096, B)
+_buf("rep0 rep1 dr es", 4096, B)
 _buf("bsh0 bsh1", 512, H)
-_buf("junk", 256, B)
+_buf("junk", 320, B)
 _buf("dm gd", 8192, B)
 _buf("g2 xp", 2048, B)
 _buf("dg", 2080, B)
@@ -51,36 +50,37 @@ _buf("ia ib ic pi", 32, I)
 _buf("ja jb jc", 8, I)
 _buf("kap", 192, U)
 _buf("wo po0 po1 ua ub", 32, U)
-_buf("sel blk w2o uc ud", 8, U)
-_buf("iw i16 wf fa fb fc bc", 32, F)
+_buf("sel blk w2o", 8, U)
+_buf("iw i16 wf fa fb fc", 32, F)
 _buf("zw", 64, F)
 _buf("old tgt dpos epos", 96, F)
-_buf("cumw sum", 40, F)
-_buf("fw", 40, B)
+_buf("cumw bc", 40, F)
+_buf("fw fs", 40, B)
+_buf("tg2 f2 o2", 16, F)
+_buf("uc", 16, U)
 _buf("gw", 32, B)
 _buf("mh dw vw", 32, H)
 _buf("col", 8, F)
-_buf("acc bj ga gb sf tg2 pd2 f2m f2d", 8, F)
+_buf("acc bj ga gb sf", 8, F)
 _buf("c2f bs2 id1 srow", 128, F)
 _buf("ec2 ea2", 128, I)
 _buf("c2o eo2", 128, U)
-_buf("mv2 mt2 dd2 ee2 cmp b1 tri ust idh idn idb one c4k", 128, B)
+_buf("mv2 mt2 dd2 ee2 cmp b1 tri ust idh idn idb one", 128, B)
 _buf("zs2", 128, H)
 _buf("m0p m0n", 144, B)
-_buf("g8", 8, B)
+_buf("g8 g8p g8n", 8, B)
 _buf("pK pX0 pX1 pG pS pU pB pF", 512, F, P_)
 SEMAPHORES = ["cv", "cs", "cp", "cg"] + ["d%d" % i for i in range(40)] + ["rl%d" % i for i in range(9)] + ["ar%d" % i for i in range(9)]
 BIG = float(2 ** 25)
 SIZE = {F: 4, I: 4, B: 2, H: 2, U: 2}
-SEARCH = ("vvvvswwswwswwsww", "vvvvvvvvvvvvssss", "vvvvvvvvvvvvssss")
-KEYS = ((0, 1, 2, 3), (0, 3, 1, 2), (0, 3, 1, 2))
+SEARCH = ("vvvvvvvvssssssss", "rrrrrrrrssssssss", "rrrrrrrrssssssss")
+KEYS = ((0, 2, 1, 3), (2, 3, 0, 1), (2, 3, 0, 1))
 ASK = "vsvv"
-REP = 6144
-DWHO = ("ssssssss", "ssssssss", "ssssssss")
+DWHO = ("ssssvsvs", "ssssssss", "ssssssss")
 EWHO = ("svsvsvss", "svsvsvss", "svsvsvss")
-CY, GAT, SCA, HOP = 0.00092, 1.5, 3.5, 0.1
+CY, GAT, SCA, HOP = 0.00092, 1.5, 3.5, 0.14
 ORDER = []
-PASSES = 4
+PASSES = 12
 
 
 def arrange(ops):
@@ -132,12 +132,12 @@ def arrange(ops):
     for i in range(n - 1, -1, -1):
         rank[i] = ops[i]["cost"] + max([tail[i]] + [rank[j] + gap for j, gap in fwd[i]])
     best = None
-    for _ in range(PASSES):
+    for p in range(PASSES):
         order, end = place(fwd, bwd, rank, [0.0] * n)
         span = max(e + t for e, t in zip(end, tail))
         if best is None or span < best[0]:
             best = (span, order)
-        rank = place(bwd, fwd, end, tail)[1]
+        rank = [r + 0.3 * ((i * 7919 + p * 104729) % 1000) / 1000 for i, r in enumerate(place(bwd, fwd, end, tail)[1])]
     return best[1]
 
 
@@ -197,7 +197,7 @@ def rank_program(g, core, T, topo):
         if sem is None:
             sem = "d%d" % nsem[0]
             nsem[0] += 1
-        lastdma[q] = emit(q, lambda e: e.dma_start(out, in_), R, W, 0.06, sem=sem, n=16, tot=tot or 16, lat=2.0 + kb / 200,
+        lastdma[q] = emit(q, lambda e: e.dma_start(out, in_), R, W, 0.06, sem=sem, n=16, tot=tot or 16, lat=1.0 + kb / 330,
                           after=[lastdma[q]] if q in lastdma else [])
 
     def ind(win, off):
@@ -303,8 +303,8 @@ def rank_program(g, core, T, topo):
         a = topo.addr(to)
         out = T[dst][:, 0:1024]
         me = emit("g", lambda q: q.remote_dma(out, src[0], T.sem["ar%d" % ix], T.sem["rl%d" % ix], a[1], a[0], m), [src, X("basi")], [], 0.3,
-                  sem="rl%d" % ix, n=0, tot=len(e), lat=6.0)
-        emit("x", None, [], [X(dst)], 0.0, sem="ar%d" % ix, n=0, tot=len(e), after=[me], lat=6.5)
+                  sem="rl%d" % ix, n=0, tot=len(e), lat=4.0)
+        emit("x", None, [], [X(dst)], 0.0, sem="ar%d" % ix, n=0, tot=len(e), after=[me], lat=4.5)
 
     dma("s", T.meas[:], T.mea[:], W=[X("meas")], kb=256)
     for c in range(4):
@@ -333,7 +333,7 @@ def rank_program(g, core, T, topo):
     for n in ("mor0", "mor1"):
         ms(X(n, FAR, SH), 16384.0)
     ms(X("tl", 1024, 1032), float(FAR))
-    ms(X("cumw", 32, 40), BIG)
+    ms(X("fw", 32, 40), 1.0)
     ms(NM, 0.0)
     iota(X("pi"), [[0, 32]], 0, 1)
     iota(X("fa"), [[256, 4], [2, 8]], 0, 0)
@@ -355,6 +355,8 @@ def rank_program(g, core, T, topo):
     asel(X("tri"), [[1, 128]], OP.is_ge, 0, -1)
     asel(X("ust"), [[-1, 128]], OP.is_gt, 0, 1)
     iota(X("srow"), [[1, 128]], 0, 0)
+    ts(X("g8p"), X("g8"), 2.0, OP.mult)
+    ts(X("g8n"), X("g8"), -1.0, OP.mult)
     ts(X("m0p", 16, 144, 16), X("g8"), 1 / 2048, OP.mult)
     ts(X("m0n", 16, 144, 16), X("g8"), -1 / 2048, OP.mult)
     ts(X("ia"), X("pi"), 15, OP.bitwise_and)
@@ -399,24 +401,28 @@ def rank_program(g, core, T, topo):
             sl = X("dm", 512 * c, 512 * c + 512)
             src = ind(X("meas"), X("cdo", 32 * c, 32 * c + 32))
             how = SEARCH[t][c]
-            if how == "v":
+            if how in "vr":
                 tt(sl, src, X("rep%d" % par, 512 * c, 512 * c + 512), OP.subtract)
                 inturn()
-                act(sl, sl, AF.Abs)
+                if how == "v":
+                    act(sl, sl, AF.Abs)
+                else:
+                    ts(X("dr", 512 * c, 512 * c + 512), sl, 0.0, OP.max)
             else:
-                bank = X("pF" if t or c % 2 else "pU")
+                bank = X("pF" if c % 2 else "pB" if t else "pU")
                 j = c // 4
                 gather(how, sl, src)
                 mm(bank, X("mpt%d" % par, 128 * j, 128 * j + 128), X("xp", 512 * (c % 4), 512 * (c % 4) + 512), True, False)
                 mm(bank, X("idh"), sl, False, True)
                 act(sl, bank, AF.Abs)
         for j in KEYS[t]:
-            if True:
-                blk = X("pK", 128 * j, 128 * j + 128)
-                mm(blk, X("cdf", 128 * j, 128 * j + 128), X("id1"), True, False)
-                mm(blk, X("eq", 128 * j, 128 * j + 128), X("idb"), False, False)
+            blk = X("pK", 128 * j, 128 * j + 128)
+            mm(blk, X("cdf", 128 * j, 128 * j + 128), X("id1"), True, False)
+            mm(blk, X("eq", 128 * j, 128 * j + 128), X("idb"), False, False)
+            parts = (("dm", "g8n"), ("dr", "g8p")) if SEARCH[t][4 * j] == "r" else (("dm", "g8"),)
+            for d, f in parts:
                 for k in range(16):
-                    mm(X("pK", 128 * j + k, 128 * j + 128, 16), X("dm", 2048 * j + k, 2048 * j + 2048, 16), X("g8"), False, k == 15)
+                    mm(X("pK", 128 * j + k, 128 * j + 128, 16), X(d, 2048 * j + k, 2048 * j + 2048, 16), X(f), False, k == 15 and d == parts[-1][0])
         scan(X("ks"), X("minm"), X("pK"), BIG, OP.max, OP.min)
         ts(X("ia"), X("ks", 15, 512, 16), float(2 ** 23 - 1024), OP.min)
         ts(X("ib"), X("ia"), 2047, OP.bitwise_and)
@@ -428,11 +434,10 @@ def rank_program(g, core, T, topo):
         for c in range(4):
             cp(X("wf", 8 * c, 8 * c + 8), X("us", 8 * c + 7, 256, 32))
         cp(X("wo"), X("wf"))
-        cp(X("ia"), X("wf"))
-        ts(X("ib"), X("ia"), 1, OP.bitwise_and)
-        ts(X("fa"), X("ib"), -2.0, OP.mult, 1.0, OP.add)
-        tt(X("fb"), X("fa"), X("wf"), OP.add)
-        tt(X("dw"), X("fb"), X("old", 32 * t, 32 * t + 32), OP.subtract)
+        ts(X("ia"), X("wf"), 0.5, OP.mult, -0.25, OP.add)
+        ts(X("fa"), X("ia"), 4.0, OP.mult, 1.0, OP.add)
+        tt(X("fb"), X("wf"), X("old", 32 * t, 32 * t + 32), OP.add)
+        tt(X("dw"), X("fa"), X("fb"), OP.subtract)
 
     flip = [0]
 
@@ -455,19 +460,23 @@ def rank_program(g, core, T, topo):
 
     send(X("meas"), "mq0", 0, 0)
     kap(0, 0)
-    for par in range(2):
+
+    def meanings(par, bank):
         mvp = "mvp%d" % par
-        ts(X("po%d" % par), X("fa"), P16, OP.add, float(par), OP.add)
         act(X(mvp), ind(X("meas"), X("po%d" % par)), AF.Copy)
-        for j in range(4):
-            mm(X("pX%d" % par, 128 * j, 128 * j + 128), X(mvp, 128 * j, 128 * j + 128), X("idn"), True, True)
-        act(X("mpt%d" % par), X("pX%d" % par), AF.Copy)
-        lo = 2048 if par == 0 else 0
-        for c in range(lo // 1024):
+        for j in range(2):
+            mm(X(bank, 128 * j, 128 * j + 128), X(mvp, 256 + 128 * j, 384 + 128 * j), X("idn"), True, True)
+        act(X("mpt%d" % par, 256, 512), X(bank, 0, 256), AF.Copy)
+        for c in range(4 * (1 - par)):
             cp(X("zsp", 0, 1024, 16), X(mvp, 64 * c, 64 * c + 64))
             scan(X("rep0", 1024 * c, 1024 * c + 1024), X("rm"), X("zsp"), 0.0, OP.mult, OP.add)
-        for k in range(16):
-            gcopy(X("rep%d" % par, lo + k, REP, 16), X(mvp, lo // 16, REP // 16))
+        for k in range(16 * par):
+            gcopy(X("rep1", k, 4096, 16), X(mvp, 0, 256))
+
+    for par in range(2):
+        ts(X("po%d" % par), X("fa"), P16, OP.add, float(par), OP.add)
+    meanings(0, "pX0")
+    for par in range(2):
         cp(X("mvt%d" % par, 0, 512), X("meas", par, 1024, 2))
         cp(X("dro%d" % par), X("dt", par, 1024, 2))
         gcopy(X("bsh%d" % par), X("basi", par, 1024, 2))
@@ -478,6 +487,8 @@ def rank_program(g, core, T, topo):
         for b in range(16):
             mm(X("pS", 32 * t, 32 * t + 32), shift((b + t) % 16, b), X("u16", 37 * t + b, 37 * t + 512, 16), b == 0, b == 15)
     cp(X("old"), X("pS", 0, 96))
+    search(0)
+    meanings(1, "pU")
     for par in range(2):
         flags(par, X("dt", par, 1024, 2), ("pB", "pG")[par])
         ts(X("zs"), X("mvt%d" % par, 0, 512), WZ, OP.mult)
@@ -497,7 +508,6 @@ def rank_program(g, core, T, topo):
         ts(X("dpos", *w), X("iw"), 1.0 if t < 2 else 0.0, OP.mult, float(t - E0 if t < 2 else 512), OP.add)
     send(X("meas"), "mq1", 1, 3)
     send(X("meas"), "mq2", 2, 6)
-    search(0)
 
     for t in range(3):
         par = t % 2
@@ -516,20 +526,17 @@ def rank_program(g, core, T, topo):
         wrap(X("pG", 0, 32), "ee", 512, "m0p", False, True)
         ts(X("fw", 0, 32), X("pG", 0, 32), NM, OP.is_ge)
         ts(X("gw"), X("pG", 0, 32), NM, OP.is_lt)
-        mm(X("pS", 0, 32), X("b1"), X("fw", 0, 32), True, True)
-        mm(X("pS", 32, 64), X("ust"), X("fw", 0, 32), True, True)
-        scan(X("bc"), X("one", 0, 32), X("pS", 0, 32), 0.0, OP.mult, OP.add)
-        tt(X("cumw", 0, 32), X("bc"), X("pS", 32, 64), OP.subtract)
+        mm(X("pS", 0, 40), X("b1"), X("fw"), True, True)
+        mm(X("pS", 256, 296), X("ust"), X("fw"), True, True)
+        scan(X("bc"), X("one", 0, 40), X("pS", 0, 40), 0.0, OP.mult, OP.add)
+        tt(X("cumw"), X("bc"), X("pS", 256, 296), OP.subtract)
         for a in range(8):
-            act(X("junk", 32 * a, 32 * a + 32), X("bc"), AF.Sign, bias=X("bj", a, a + 1), scale=-1.0, accum=X("acc", a, a + 1))
-        ts(X("blk"), X("acc"), 0.5, OP.mult, 16.0, OP.add)
+            act(X("junk", 40 * a, 40 * a + 40), X("bc"), AF.Sign, bias=X("bj", a, a + 1), scale=-1.0, accum=X("acc", a, a + 1))
+        ts(X("blk"), X("acc"), 0.5, OP.mult, 20.0, OP.add)
         tt(X("cmp"), ind(X("cumw"), X("blk")), X("srow"), OP.is_le)
         wrap(X("pS", 64, 72), "cmp", 128)
-        ts(X("ga"), X("acc"), 32.0, OP.is_ge)
-        tt(X("ga"), X("ga"), X("iw", 0, 8), OP.mult)
-        ts(X("gb"), X("acc"), 8.0, OP.mult, 256.0, OP.add)
-        tt(X("ga"), X("ga"), X("gb"), OP.add)
-        tt(X("sf"), X("pS", 64, 72), X("ga"), OP.add)
+        act(X("gb"), X("acc"), AF.Copy, bias=320.0, scale=8.0)
+        tt(X("sf"), X("pS", 64, 72), X("gb"), OP.add)
         cp(X("sel"), X("sf"))
         tt(X("vw"), X("dw"), X("gw"), OP.mult)
         for b in range(16):
@@ -540,21 +547,21 @@ def rank_program(g, core, T, topo):
         if t < 2:
             send(X("usei"), "uq%d" % (t + 1), t + 1, 4 if t == 0 else 7)
         else:
-            gcopy(X("usef"), X("usei"))
-            dma("y", T.yu[:], T.usef[:], R=[X("usef")])
+            gcopy(X("tq0"), X("usei"))
+            dma("y", T.yu[:], T.tq0[:], R=[X("tq0")])
         new = X("dt", D0, D0 + 512) if t == 0 else X("ydb", par, 1024, 2)
         tt(X("fa"), X("fw", 0, 32), X("dpos", *w), OP.mult)
         tt(X("fb"), X("fa"), X("epos", *w), OP.add)
         cp(X("ua"), X("fb"))
         cp(new, ind(X("dt", 0, D0) if t < 2 else X("dt", E0, D0 + 512), X("ua")))
-        ts(X("fc"), X("fw", 0, 32), float(SH), OP.mult)
-        tt(X("fc"), X("fc"), X("tgt", *w), OP.add)
+        ts(X("fs", 0, 32), X("fw", 0, 32), float(SH), OP.mult)
+        tt(X("fc"), X("fs", 0, 32), X("tgt", *w), OP.add)
         cp(X("ub"), X("fc"))
         for h in range(4):
             cp(ind(X(nxt), X("ub", 8 * h, 8 * h + 8)), X(mvt, 128 * h, 128 * h + 128))
-        cp(X("c2f"), ind(X("cq"), X("sel")))
-        cp(X("c2o"), X("c2f"))
+        cp(X("c2o"), ind(X("cq"), X("sel")))
         act(X("mv2"), ind(X(mvt), X("sel")), AF.Copy)
+        act(X("c2f"), ind(X("cq"), X("sel")), AF.Copy)
         mm(X("pS", 128, 256), X("mv2"), X("idn"), True, True)
         act(X("mt2"), X("pS", 128, 256), AF.Copy)
         mm(X("pU", 0, 128), X("c2f"), X("id1"), True, False)
@@ -586,9 +593,9 @@ def rank_program(g, core, T, topo):
         wrap(X("pS", 72, 80), "zs2", 128)
         ts(X("ja"), X("pS", 72, 80), float(t), OP.add)
         ts(X("jb"), X("ja"), 3, OP.bitwise_and)
-        ts(X("ga"), X("sf"), 4.0, OP.mult)
-        tt(X("tg2"), X("ga"), X("jb"), OP.add)
-        ts(X("pd2"), X("sf"), 2.0 if t else 1.0, OP.mult, float(par), OP.add)
+        act(X("ga"), X("sf"), AF.Copy, scale=4.0)
+        tt(X("tg2", 0, 8), X("ga"), X("jb"), OP.add)
+        act(X("tg2", 8, 16), X("sf"), AF.Copy, scale=2.0 if t else 1.0, bias=float(par))
         scan(X("ks", 0, 128), X("minm", 0, 128), X("pU", 0, 128), BIG, OP.max, OP.min)
         cp(X("ja"), X("ks", 15, 128, 16))
         ts(X("jc"), X("ja"), 2047, OP.bitwise_and)
@@ -603,22 +610,20 @@ def rank_program(g, core, T, topo):
         cp(X("eo2"), X("ea2"))
         lists("svsv", mor, "eo2", "ee2", "mv2", 512, (3,))
         wrap(X("pG", 32, 40), "ee2", 128, "m0p", False, True)
-        ts(X("f2m"), X("pG", 32, 40), NM, OP.is_ge, float(SH), OP.mult)
-        ts(X("f2d"), X("pG", 32, 40), NM, OP.is_ge, 1280.0 if t else 640.0, OP.mult)
-        ts(X("fw", 32, 40), X("pG", 32, 40), NM, OP.is_ge)
-        tt(X("ga"), X("f2m"), X("tg2"), OP.add)
-        cp(X("uc"), X("ga"))
-        cp(ind(X(nxt), X("uc")), X("mv2"))
-        tt(X("gb"), X("f2d"), X("pd2"), OP.add)
-        cp(X("ud"), X("gb"))
-        cp(ind(X("ydb") if t else X("dt", D0, 2816), X("ud")), X("ea2"))
+        ts(X("f2", 0, 8), X("pG", 32, 40), NM, OP.is_ge, float(SH), OP.mult)
+        ts(X("f2", 8, 16), X("pG", 32, 40), NM, OP.is_ge, 1280.0 if t else 640.0, OP.mult)
+        tt(X("o2"), X("f2"), X("tg2"), OP.add)
+        cp(X("uc"), X("o2"))
+        cp(ind(X(nxt), X("uc", 0, 8)), X("mv2"))
+        cp(ind(X("ydb") if t else X("dt", D0, 2816), X("uc", 8, 16)), X("ea2"))
         if t < 2:
             search(t + 1)
             flags(par, new, "pB")
             send(X("tl", 0, 1024), "tq%d" % (t + 1), t + 1, 5 if t == 0 else 8)
-            mm(X("pS", 80, 120), X("one"), X("fw"), True, True)
-            emit("v", lambda e: e.tensor_reduce(TOT[0], T.pS[:, 80:120], AxisListType.X, OP.add), [X("pS", 80, 120)], [TOT], 64 * CY)
-            ts(X("ja", 0, 1), TOT, -1.0, OP.mult)
+            act(X("fs", 32, 40), X("f2", 0, 8), AF.Copy)
+            mm(X("pS", 80, 120), X("one"), X("fs"), True, True)
+            act(X("bc"), X("pS", 80, 120), AF.Copy, accum=TOT)
+            ts(X("ja", 0, 1), TOT, -1.0 / SH, OP.mult)
             ts(X("jb", 0, 1), X("ja", 0, 1), 127, OP.bitwise_and)
             ts(NM, X("jb", 0, 1), -1.0, OP.mult)
         if t == 0:

@@ -2,8 +2,8 @@ from concourse.mybir import AluOpType as OP, ActivationFunctionType as AF
 
 S_, P_ = "sbuf", "psum"
 F, B, H, I, U = "float32", "bfloat16", "float16", "int32", "uint16"
-FAR = 2048
-SH = 2064
+SH = 2048
+FAR = 4608
 E0, D0 = 1024, 1536
 SCRATCH, PART = {}, {}
 
@@ -24,35 +24,32 @@ _buf("bw", 128, I)
 _buf("b15", 994, I)
 _buf("basi usei uq0 uq1 uq2", 1024, I)
 _buf("dt", 2816, I)
-_buf("meas mq0 mq1 mq2 rm zsp la1 la2", 1024, B)
+_buf("meas mq0 mq1 mq2", 1024, B)
 _buf("mor0 mor1", 4624, B)
 _buf("tq0 tq1 tq2", 1024, F)
 _buf("tl", 1032, F)
 _buf("ydb", 2560, F)
 _buf("mvt0 mvt1 dd", 640, B)
-_buf("mvp0 mvp1 mpt0 mpt1 eq ee neq minm vrh vrl0 vrl1", 512, B)
+_buf("mvp0 mvp1 mpt0 mpt1 eq ee neq", 512, B)
 _buf("bst0 bst1 cq", 640, F)
+_buf("bsh0 bsh1", 512, H)
+_buf("u16", 592, H)
 _buf("dro0 dro1 cdo eo", 512, U)
 _buf("rep0 rep1 dr es", 4096, B)
-_buf("bsh0 bsh1", 512, H)
-_buf("junk", 320, B)
 _buf("dm gd", 8192, B)
-_buf("g2 xp", 2048, B)
-_buf("dg", 2080, B)
+_buf("g2", 2048, B)
 _buf("cdf ks", 512, F)
 _buf("ec", 512, I)
-_buf("zs", 512, H)
-_buf("u16", 592, H)
-_buf("um", 256, H)
 _buf("us", 256, F)
-_buf("m8 m8r", 256, B)
-_buf("ia ib ic pi", 32, I)
+_buf("junk", 320, B)
+_buf("ia ib pi", 32, I)
 _buf("ja jb jc", 8, I)
 _buf("kap", 192, U)
+_buf("kin", 192, I)
+_buf("zin", 96, I)
 _buf("wo po0 po1 ua ub", 32, U)
 _buf("sel blk w2o", 8, U)
-_buf("iw i16 wf fa fb fc", 32, F)
-_buf("zw", 64, F)
+_buf("i16 wf fa fb fc ha hb", 32, F)
 _buf("old tgt dpos epos", 96, F)
 _buf("cumw bc", 40, F)
 _buf("fw fs", 40, B)
@@ -61,13 +58,20 @@ _buf("uc", 16, U)
 _buf("gw", 32, B)
 _buf("mh dw vw", 32, H)
 _buf("col", 8, F)
-_buf("acc bj ga gb sf", 8, F)
-_buf("c2f bs2 id1 srow", 128, F)
+_buf("acc bj ga sf", 8, F)
+_buf("gb", 8, B)
+_buf("c2f bs2", 128, F)
 _buf("ec2 ea2", 128, I)
 _buf("c2o eo2", 128, U)
-_buf("mv2 mt2 dd2 ee2 cmp b1 tri ust idh idn idb one", 128, B)
-_buf("zs2", 128, H)
-_buf("m0p m0n", 144, B)
+_buf("mv2 mt2 dd2 ee2 cmp", 128, B)
+_buf("rm zsp la1 la2", 1024, B)
+_buf("minm vrh vrl0 vrl1", 512, B)
+_buf("xp", 2048, B)
+_buf("dg", 2080, B)
+_buf("m8 m8r", 256, B)
+_buf("id1 srow", 128, F)
+_buf("b1 tri ust idh idn idb one", 128, B)
+_buf("m0p m0n m0w", 144, B)
 _buf("g8 g8p g8n", 8, B)
 _buf("pK pX0 pX1 pG pS pU pB pF", 512, F, P_)
 SEMAPHORES = ["cv", "cs", "cp", "cg"] + ["d%d" % i for i in range(40)] + ["rl%d" % i for i in range(9)] + ["ar%d" % i for i in range(9)]
@@ -76,11 +80,11 @@ SIZE = {F: 4, I: 4, B: 2, H: 2, U: 2}
 SEARCH = ("vvvvvvvvssssssss", "rrrrrrrrssssssss", "rrrrrrrrssssssss")
 KEYS = ((0, 2, 1, 3), (2, 3, 0, 1), (2, 3, 0, 1))
 ASK = "vsvv"
-DWHO = ("ssssvsvs", "ssssssss", "ssssssss")
+DWHO = ("ssvsvsvs", "ssssssss", "ssssssss")
 EWHO = ("svsvsvss", "svsvsvss", "svsvsvss")
-CY, GAT, SCA, HOP = 0.00092, 1.5, 3.5, 0.14
+CY, GAT, SCA, HOP = 0.00085, 1.56, 3.8, 0.17
 ORDER = []
-PASSES = 12
+PASSES = 16
 
 
 def arrange(ops):
@@ -152,9 +156,9 @@ def rank_program(g, core, T, topo):
         lo, hi = at + lo, at + (n if hi is None else hi)
         return (T[name][:, lo:hi] if st == 1 else T[name][:, lo:hi:st], name, lo, hi, st)
 
-    def X0(name, lo=0, hi=None):
-        hi = SCRATCH[name][1][1] if hi is None else hi
-        return (T[name][0:1, lo:hi], name, lo, hi, 1)
+    def X0(name):
+        hi = SCRATCH[name][1][1]
+        return (T[name][0:1, 0:hi], name, 0, hi, 1)
 
     def cnt(v):
         return 16 * cnt(v[2]) if len(v) == 3 else len(range(v[2], v[3], v[4]))
@@ -248,14 +252,7 @@ def rank_program(g, core, T, topo):
         else:
             emit("s", lambda e: e.activation(out[0], a[0], func, bias=val(bias), scale=scale), rd(a, bias), [out], cost(a, per=1))
 
-    def gather(who, out, src):
-        if who == "s":
-            act(out, src, AF.Copy)
-        else:
-            cp(out, src)
-        inturn()
-
-    turn = {}
+    turn, kind = {}, [0]
 
     def inturn():
         me = len(ops) - 1
@@ -264,7 +261,12 @@ def rank_program(g, core, T, topo):
             ops[me]["deps"].setdefault(turn[key], False)
         turn[key] = me
 
-    kind = [0]
+    def gather(who, out, src):
+        if who == "s":
+            act(out, src, AF.Copy)
+        else:
+            cp(out, src)
+        inturn()
 
     def mm(out, l, r, start, stop):
         c = max(min(64, cnt(l)), cnt(r)) * (4 if SCRATCH[l[1]][2] == F else 1) * CY
@@ -313,12 +315,13 @@ def rank_program(g, core, T, topo):
     dma("y", T.dt[:, 0:1024], T.der[:], W=[X("dt", 0, 1024)], kb=1280)
     dma("y", T.mor0[:, 0:2048], T.mor[:], W=[X("mor0", 0, 2048)], kb=1792)
     dma("y", T.basi[:], T.bas[:], W=[X("basi")], kb=2304)
-    dma("y", T.mor1[:, 0:2048], T.mor[:], W=[X("mor1", 0, 2048)], kb=2816)
+    dma("y", T.mor0[:, 2048:4096], T.mor[:], W=[X("mor0", 2048, 4096)], kb=2816)
+    dma("y", T.mor1[:, 0:2048], T.mor[:], W=[X("mor1", 0, 2048)], kb=3300)
     for b in range(16):
-        dma("y", T.b15[b::16, 0:994], T.bas[15::16, 2 * b:2 * b + 994], W=[X("b15")] if b == 15 else [], sem="d39", tot=256, kb=3300)
+        dma("y", T.b15[b::16, 0:994], T.bas[15::16, 2 * b:2 * b + 994], W=[X("b15")] if b == 15 else [], sem="d39", tot=256, kb=3800)
 
-    PK, P16, PEN, WZ, NM, TOT = [X("col", k, k + 1) for k in range(6)]
-    for n, v in (("rm", 1), ("zsp", 0), ("g8", 2048), ("id1", 1), ("idb", 2 ** 23), ("idh", 1), ("idn", -1), ("minm", 0), ("la1", 1), ("la2", 1), ("m8", 1),
+    PK, P16, PEN, WZ, NM, TOT, P4 = [X("col", k, k + 1) for k in range(7)]
+    for n, v in (("rm", 1), ("zsp", 0), ("g8", 2048), ("id1", 1), ("idb", 2 ** 23), ("idh", 1), ("idn", -1), ("minm", 0), ("m8", 1),
                  ("m8r", 1), ("b1", 1), ("tri", 1), ("ust", 1), ("one", 1), ("m0p", 0), ("m0n", 0)):
         ms(X(n), float(v))
     ms(X("rm", 0, 1024, 16), 0.0)
@@ -329,10 +332,10 @@ def rank_program(g, core, T, topo):
     for n in ("mvt0", "mvt1", "dd", "cq"):
         ms(X(n, 512, 640), 0.0)
     for n in ("bst0", "bst1"):
-        ms(X(n, 512, 640), -4096.0)
+        ms(X(n, 512, 640), -2048.0)
     for n in ("mor0", "mor1"):
-        ms(X(n, FAR, SH), 16384.0)
-    ms(X("tl", 1024, 1032), float(FAR))
+        ms(X(n, 4096, 4624), 16384.0)
+    ms(X("tl", 1024, 1032), float(FAR - 2048))
     ms(X("fw", 32, 40), 1.0)
     ms(NM, 0.0)
     iota(X("pi"), [[0, 32]], 0, 1)
@@ -347,9 +350,10 @@ def rank_program(g, core, T, topo):
     for par in range(2):
         iota(X0("vrl%d" % par), [[0, 4], [2, 8], [0, 16]], par, 0)
     for x in range(8):
-        asel(X("la1", 128 * x, 128 * x + 128), [[0, 8], [-1, 2], [-16, 8]], OP.is_equal, -2 * x, 1)
-    asel(X("la2"), [[-16, 8], [0, 8], [-1, 16]], OP.is_equal, 0, 1)
+        asel(X("la1", 128 * x, 128 * x + 128), [[0, 8], [-1, 2], [-16, 8]], OP.is_equal, -2 * x, 1, X("one"))
+        asel(X("la2", 128 * x, 128 * x + 128), [[0, 8], [-1, 16]], OP.is_equal, -16 * x, 1, X("one"))
     same(X("m8"), [[0, 32]], [])
+    ts(X("m8"), X("m8"), 4096.0, OP.mult, -4096.0, OP.add)
     for n in ("b1", "tri", "ust"):
         same(X(n), [], [[0, 16]])
     asel(X("tri"), [[1, 128]], OP.is_ge, 0, -1)
@@ -365,21 +369,18 @@ def rank_program(g, core, T, topo):
     for b in range(16):
         ts(X("dg", 16 + 128 * b, 144 + 128 * b), X("idh"), X("fc", b, b + 1), OP.mult)
     ts(P16, PK, 16.0, OP.mult)
+    ts(P4, PK, 4.0, OP.mult)
     ts(PEN, PK, 15.0, OP.is_lt, 8192.0, OP.mult)
-    ts(X("ib", 0, 1), X("ia", 0, 1), 1, OP.add)
-    ts(X("ic", 0, 1), X("ib", 0, 1), 3, OP.bitwise_and)
-    cp(WZ, X("ic", 0, 1))
-    ts(X("iw"), X("i16"), PK, OP.add)
-    ts(X("bj"), X("iw", 0, 8), 0.5, OP.add)
+    ts(WZ, PK, 1.0, OP.add)
+    ts(X("m0w"), X("m0p"), WZ, OP.mult)
+    ts(X("bj"), X("i16", 0, 8), PK, OP.add, 0.5, OP.add)
 
-    def kap(t, nat):
-        src = X("b15", t % 2, 994, 32) if nat else X("bw", t % 2, 64, 2)
-        ts(X("ib"), src, 97 * t, OP.add)
-        ts(X("ic"), X("ib"), 1023, OP.bitwise_and)
-        cp(KAP(t, nat), X("ic"))
-
-    def KAP(t, nat):
-        return X("kap", 64 * t + 32 * nat, 64 * t + 32 * nat + 32)
+    def kap(lo, hi):
+        for j in range(lo, hi):
+            t = j // 2
+            ts(X("kin", 32 * j, 32 * j + 32), X("b15", t % 2, 994, 32) if j % 2 else X("bw", t % 2, 64, 2), 97 * t, OP.add)
+        ts(X("kin", 32 * lo, 32 * hi), X("kin", 32 * lo, 32 * hi), 1023, OP.bitwise_and)
+        cp(X("kap", 32 * lo, 32 * hi), X("kin", 32 * lo, 32 * hi))
 
     def flags(par, der, bank):
         mm(X(bank), X("idh"), X("bsh%d" % par), True, True)
@@ -427,13 +428,13 @@ def rank_program(g, core, T, topo):
         ts(X("ia"), X("ks", 15, 512, 16), float(2 ** 23 - 1024), OP.min)
         ts(X("ib"), X("ia"), 2047, OP.bitwise_and)
         cp(X("mh"), X("ib"))
+        mm(X("pF", 0, 256), X("idh"), X("m8"), True, False)
         for x in range(8):
-            mm(X("pF", 32 * x, 32 * x + 32), X("la1", 128 * x, 128 * x + 128), X("mh"), True, True)
-        tt(X("um"), X("pF", 0, 256), X("m8"), OP.mult)
-        scan(X("us"), X("m8r"), X("um"), 0.0, OP.mult, OP.add)
+            mm(X("pF", 32 * x, 32 * x + 32), X("la1", 128 * x, 128 * x + 128), X("mh"), False, x == 7)
+        scan(X("us"), X("m8r"), X("pF", 0, 256), 0.0, OP.mult, OP.max)
         for c in range(4):
-            cp(X("wf", 8 * c, 8 * c + 8), X("us", 8 * c + 7, 256, 32))
-        cp(X("wo"), X("wf"))
+            cp(X("wo", 8 * c, 8 * c + 8), X("us", 8 * c + 7, 256, 32))
+        cp(X("wf"), X("wo"))
         ts(X("ia"), X("wf"), 0.5, OP.mult, -0.25, OP.add)
         ts(X("fa"), X("ia"), 4.0, OP.mult, 1.0, OP.add)
         tt(X("fb"), X("wf"), X("old", 32 * t, 32 * t + 32), OP.add)
@@ -441,13 +442,13 @@ def rank_program(g, core, T, topo):
 
     flip = [0]
 
-    def lists(who, mor, offs, dist, mv, n, ends):
+    def lists(who, win, offs, dist, mv, n, ends):
         lo = 0
         kind[0] = "lists"
         for c, w in enumerate(who):
             k = n // 16
             a = X("gd", n * c, n * c + n)
-            gather(w, a, ind(X(mor, 0, SH), X(offs, k * c, k * c + k)))
+            gather(w, a, ind(win, X(offs, k * c, k * c + k)))
             e = (n * c) % 4096
             scan(X("es", e, e + n), X("rm", 0, n), a, 0.0, OP.mult, OP.max)
             px = "pX%d" % flip[0]
@@ -458,31 +459,39 @@ def rank_program(g, core, T, topo):
                 lo = k * c + k
                 flip[0] ^= 1
 
-    send(X("meas"), "mq0", 0, 0)
-    kap(0, 0)
-
     def meanings(par, bank):
         mvp = "mvp%d" % par
         act(X(mvp), ind(X("meas"), X("po%d" % par)), AF.Copy)
         for j in range(2):
             mm(X(bank, 128 * j, 128 * j + 128), X(mvp, 256 + 128 * j, 384 + 128 * j), X("idn"), True, True)
         act(X("mpt%d" % par, 256, 512), X(bank, 0, 256), AF.Copy)
-        for c in range(4 * (1 - par)):
+        for c in range(2 * (1 - par)):
             cp(X("zsp", 0, 1024, 16), X(mvp, 64 * c, 64 * c + 64))
             scan(X("rep0", 1024 * c, 1024 * c + 1024), X("rm"), X("zsp"), 0.0, OP.mult, OP.add)
-        for k in range(16 * par):
-            gcopy(X("rep1", k, 4096, 16), X(mvp, 0, 256))
+        lo = 2048 * (1 - par)
+        for k in range(16):
+            gcopy(X("rep%d" % par, lo + k, 4096, 16), X(mvp, lo // 16, 256))
 
+    def targets(par):
+        wrap(X("pS", 96, 128), "mvt%d" % par, 512, "m0w")
+        for t in range(par, 3, 2):
+            w = (32 * t, 32 * t + 32)
+            ts(X("zin", *w), X("pS", 96, 128), float(t), OP.add)
+            ts(X("zin", *w), X("zin", *w), 3, OP.bitwise_and)
+            tt(X("tgt", *w), X("tgt", *w), X("zin", *w), OP.add)
+
+    send(X("meas"), "mq0", 0, 0)
+    kap(0, 1)
     for par in range(2):
         ts(X("po%d" % par), X("fa"), P16, OP.add, float(par), OP.add)
     meanings(0, "pX0")
     for par in range(2):
-        cp(X("mvt%d" % par, 0, 512), X("meas", par, 1024, 2))
-        cp(X("dro%d" % par), X("dt", par, 1024, 2))
+        gcopy(X("mvt%d" % par, 0, 512), X("meas", par, 1024, 2))
+        (gcopy if par else cp)(X("dro%d" % par), X("dt", par, 1024, 2))
         gcopy(X("bsh%d" % par), X("basi", par, 1024, 2))
-        ts(X("bst%d" % par, 0, 512), X("basi", par, 1024, 2), -4096.0, OP.add)
+        ts(X("bst%d" % par, 0, 512), X("basi", par, 1024, 2), -2048.0, OP.add)
     send(X("usei"), "uq0", 0, 1)
-    cp(X("u16"), X("usei", 0, 592))
+    gcopy(X("u16"), X("usei", 0, 592))
     for t in range(3):
         for b in range(16):
             mm(X("pS", 32 * t, 32 * t + 32), shift((b + t) % 16, b), X("u16", 37 * t + b, 37 * t + 512, 16), b == 0, b == 15)
@@ -491,21 +500,17 @@ def rank_program(g, core, T, topo):
     meanings(1, "pU")
     for par in range(2):
         flags(par, X("dt", par, 1024, 2), ("pB", "pG")[par])
-        ts(X("zs"), X("mvt%d" % par, 0, 512), WZ, OP.mult)
-        wrap(X("pS", 96 + 32 * par, 128 + 32 * par), "zs", 512)
-    cp(X("zw"), X("pS", 96, 160))
     send(X("tl", 0, 1024), "tq0", 0, 2)
-    for t in range(3):
-        w = (32 * t, 32 * t + 32)
-        if t:
-            kap(t, 0)
-        kap(t, 1)
-        ts(X("ia"), X("zw", 32 * (t % 2), 32 * (t % 2) + 32), float(t), OP.add)
-        ts(X("ib"), X("ia"), 3, OP.bitwise_and)
-        ts(X("fb"), X("iw"), 4.0, OP.mult)
-        tt(X("tgt", *w), X("fb"), X("ib"), OP.add)
-        ts(X("epos", *w), X("iw"), float(E0 if t < 2 else 0), OP.add)
-        ts(X("dpos", *w), X("iw"), 1.0 if t < 2 else 0.0, OP.mult, float(t - E0 if t < 2 else 512), OP.add)
+    kap(1, 6)
+    iota(X("tgt"), [[0, 3], [64, 32]], 0, 0)
+    ts(X("tgt"), X("tgt"), P4, OP.add)
+    targets(0)
+    iota(X("epos", 0, 64), [[0, 2], [16, 32]], E0, 0)
+    iota(X("epos", 64, 96), [[16, 32]], 0, 0)
+    ts(X("epos"), X("epos"), PK, OP.add)
+    iota(X("dpos", 0, 64), [[1, 2], [16, 32]], -E0, 0)
+    ts(X("dpos", 0, 64), X("dpos", 0, 64), PK, OP.add)
+    ms(X("dpos", 64, 96), 512.0)
     send(X("meas"), "mq1", 1, 3)
     send(X("meas"), "mq2", 2, 6)
 
@@ -514,15 +519,16 @@ def rank_program(g, core, T, topo):
         mvt, bst, mor, nxt = "mvt%d" % par, "bst%d" % par, "mor%d" % par, "mor%d" % (1 - par)
         w = (32 * t, 32 * t + 32)
         if t:
-            dma("y", T[nxt][:, 0:2048], T[mor][:, 0:2048], R=[X(mor, 0, 2048)], W=[X(nxt, 0, 2048)])
-        lists(DWHO[t], mor, "dro%d" % par, "dd", mvt, 1024, (3, 7))
+            dma("y", T[mor][:, 2048:4096], T[mor][:, 0:2048], R=[X(mor, 0, 2048)], W=[X(mor, 2048, 4096)])
+            dma("y", T[nxt][:, 0:2048], T[mor][:, 0:2048], R=[X(mor, 0, 2048)], W=[X(nxt, 0, 2048)], kb=1024)
+        lists(DWHO[t], X(mor, 0, 2048), "dro%d" % par, "dd", mvt, 1024, (3, 7))
         wrap(X("pG", 0, 32), "dd", 512, "m0n", True, False)
         for h in range(2):
             l = (256 * h, 256 * h + 256)
             tt(X("ec", *l), ind(X("tl"), X("wo", 16 * h, 16 * h + 16)), X(bst, *l), OP.max)
-            ts(X("dt", E0 + l[0], E0 + l[1]), X("ec", *l), 4095, OP.bitwise_and)
-            cp(X("eo", *l), X("dt", E0 + l[0], E0 + l[1]))
-        lists(EWHO[t], mor, "eo", "ee", mvt, 1024, (3, 6, 7))
+            ts(X("eo", *l), X("ec", *l), 2048.0, OP.add)
+        ts(X("dt", E0, E0 + 512), X("ec"), 2047, OP.bitwise_and)
+        lists(EWHO[t], X(mor), "eo", "ee", mvt, 1024, (3, 6, 7))
         wrap(X("pG", 0, 32), "ee", 512, "m0p", False, True)
         ts(X("fw", 0, 32), X("pG", 0, 32), NM, OP.is_ge)
         ts(X("gw"), X("pG", 0, 32), NM, OP.is_lt)
@@ -534,15 +540,16 @@ def rank_program(g, core, T, topo):
             act(X("junk", 40 * a, 40 * a + 40), X("bc"), AF.Sign, bias=X("bj", a, a + 1), scale=-1.0, accum=X("acc", a, a + 1))
         ts(X("blk"), X("acc"), 0.5, OP.mult, 20.0, OP.add)
         tt(X("cmp"), ind(X("cumw"), X("blk")), X("srow"), OP.is_le)
-        wrap(X("pS", 64, 72), "cmp", 128)
         act(X("gb"), X("acc"), AF.Copy, bias=320.0, scale=8.0)
-        tt(X("sf"), X("pS", 64, 72), X("gb"), OP.add)
-        cp(X("sel"), X("sf"))
+        mm(X("pS", 64, 72), X("idh"), X("gb"), True, False)
+        wrap(X("pS", 64, 72), "cmp", 128, start=False)
+        cp(X("sel"), X("pS", 64, 72))
+        cp(X("sf"), X("pS", 64, 72))
         tt(X("vw"), X("dw"), X("gw"), OP.mult)
         for b in range(16):
             mm(X("pB", b, 512, 16), shift(b, (b + t) % 16), X("vw"), True, True)
         us = X("usei", 37 * t, 37 * t + 512)
-        act(X("cq", 0, 512), ind(X("uq%d" % t), KAP(t, 1)), AF.Copy)
+        act(X("cq", 0, 512), ind(X("uq%d" % t), X("kap", 64 * t + 32, 64 * t + 64)), AF.Copy)
         tt(us, X("pB"), us, OP.add)
         if t < 2:
             send(X("usei"), "uq%d" % (t + 1), t + 1, 4 if t == 0 else 7)
@@ -550,15 +557,15 @@ def rank_program(g, core, T, topo):
             gcopy(X("tq0"), X("usei"))
             dma("y", T.yu[:], T.tq0[:], R=[X("tq0")])
         new = X("dt", D0, D0 + 512) if t == 0 else X("ydb", par, 1024, 2)
-        tt(X("fa"), X("fw", 0, 32), X("dpos", *w), OP.mult)
-        tt(X("fb"), X("fa"), X("epos", *w), OP.add)
-        cp(X("ua"), X("fb"))
+        tt(X("ha"), X("fw", 0, 32), X("dpos", *w), OP.mult)
+        tt(X("hb"), X("ha"), X("epos", *w), OP.add)
+        cp(X("ua"), X("hb"))
         cp(new, ind(X("dt", 0, D0) if t < 2 else X("dt", E0, D0 + 512), X("ua")))
         ts(X("fs", 0, 32), X("fw", 0, 32), float(SH), OP.mult)
         tt(X("fc"), X("fs", 0, 32), X("tgt", *w), OP.add)
         cp(X("ub"), X("fc"))
         for h in range(4):
-            cp(ind(X(nxt), X("ub", 8 * h, 8 * h + 8)), X(mvt, 128 * h, 128 * h + 128))
+            cp(ind(X(nxt, 0, FAR), X("ub", 8 * h, 8 * h + 8)), X(mvt, 128 * h, 128 * h + 128))
         cp(X("c2o"), ind(X("cq"), X("sel")))
         act(X("mv2"), ind(X(mvt), X("sel")), AF.Copy)
         act(X("c2f"), ind(X("cq"), X("sel")), AF.Copy)
@@ -589,8 +596,7 @@ def rank_program(g, core, T, topo):
         act(X("dd2"), ind(X("dd"), X("sel")), AF.Copy)
         act(X("bs2"), ind(X(bst), X("sel")), AF.Copy)
         wrap(X("pG", 32, 40), "dd2", 128, "m0n", True, False)
-        ts(X("zs2"), X("mv2"), WZ, OP.mult)
-        wrap(X("pS", 72, 80), "zs2", 128)
+        wrap(X("pS", 72, 80), "mv2", 128, "m0w")
         ts(X("ja"), X("pS", 72, 80), float(t), OP.add)
         ts(X("jb"), X("ja"), 3, OP.bitwise_and)
         act(X("ga"), X("sf"), AF.Copy, scale=4.0)
@@ -600,21 +606,21 @@ def rank_program(g, core, T, topo):
         cp(X("ja"), X("ks", 15, 128, 16))
         ts(X("jc"), X("ja"), 2047, OP.bitwise_and)
         cp(X("mh", 0, 8), X("jc"))
+        mm(X("pU", 256, 320), X("idh"), X("m8", 0, 64), True, False)
         for x in range(8):
-            mm(X("pU", 256 + 8 * x, 264 + 8 * x), X("la2", 128 * x, 128 * x + 128), X("mh", 0, 8), True, True)
-        tt(X("um", 0, 64), X("pU", 256, 320), X("m8", 0, 64), OP.mult)
-        scan(X("us", 0, 64), X("m8r", 0, 64), X("um", 0, 64), 0.0, OP.mult, OP.add)
+            mm(X("pU", 256 + 8 * x, 264 + 8 * x), X("la2", 128 * x, 128 * x + 128), X("mh", 0, 8), False, x == 7)
+        scan(X("us", 0, 64), X("m8r", 0, 64), X("pU", 256, 320), 0.0, OP.mult, OP.max)
         cp(X("w2o"), X("us", 7, 64, 8))
         tt(X("ec2"), ind(X("tq%d" % t), X("w2o")), X("bs2"), OP.max)
-        ts(X("ea2"), X("ec2"), 4095, OP.bitwise_and)
-        cp(X("eo2"), X("ea2"))
-        lists("svsv", mor, "eo2", "ee2", "mv2", 512, (3,))
+        ts(X("eo2"), X("ec2"), 2048.0, OP.add)
+        ts(X("ea2"), X("ec2"), 2047, OP.bitwise_and)
+        lists("svsv", X(mor), "eo2", "ee2", "mv2", 512, (3,))
         wrap(X("pG", 32, 40), "ee2", 128, "m0p", False, True)
         ts(X("f2", 0, 8), X("pG", 32, 40), NM, OP.is_ge, float(SH), OP.mult)
         ts(X("f2", 8, 16), X("pG", 32, 40), NM, OP.is_ge, 1280.0 if t else 640.0, OP.mult)
         tt(X("o2"), X("f2"), X("tg2"), OP.add)
         cp(X("uc"), X("o2"))
-        cp(ind(X(nxt), X("uc", 0, 8)), X("mv2"))
+        cp(ind(X(nxt, 0, FAR), X("uc", 0, 8)), X("mv2"))
         cp(ind(X("ydb") if t else X("dt", D0, 2816), X("uc", 8, 16)), X("ea2"))
         if t < 2:
             search(t + 1)
@@ -627,18 +633,17 @@ def rank_program(g, core, T, topo):
             ts(X("jb", 0, 1), X("ja", 0, 1), 127, OP.bitwise_and)
             ts(NM, X("jb", 0, 1), -1.0, OP.mult)
         if t == 0:
-            cp(X("dro0"), new)
+            gcopy(X("dro0"), new)
+            targets(1)
     dma("s", T.ym[:], T.mor1[:, 0:2048], R=[X("mor1", 0, 2048)])
     dma("y", T.yd[:], T.ydb[:, 0:1024], R=[X("ydb", 0, 1024)])
 
     if not ORDER:
         ORDER.extend(arrange(ops))
-    order = ORDER
-
     queue = {"v": g.vector, "s": g.scalar, "p": g.tensor, "g": g, "y": g.sync}
     clock = {q: {} for q in queue}
     total = {}
-    for pos, i in enumerate(order):
+    for pos, i in enumerate(ORDER):
         o = ops[i]
         q = o["q"]
         o["pos"] = pos

from concourse.mybir import AluOpType as OP, ActivationFunctionType as AF

S_, P_ = "sbuf", "psum"
F, B, H, I, U = "float32", "bfloat16", "float16", "int32", "uint16"
SH = 2048
FAR = 4608
E0, D0 = 1024, 1536
SCRATCH, PART = {}, {}


def _buf(names, n, d, where=S_):
    for x in names.split():
        if n > 100:
            SCRATCH[x] = (where, [128, n], d)
            PART[x] = (x, 0, n)
        else:
            home = "small_" + d
            at = SCRATCH[home][1][1] if home in SCRATCH else 0
            SCRATCH[home] = (where, [128, at + (n + 15) // 16 * 16], d)
            PART[x] = (home, at, n)


_buf("bw", 128, I)
_buf("b15", 994, I)
_buf("basi usei uq0 uq1 uq2", 1024, I)
_buf("dt", 2816, I)
_buf("meas mq0 mq1 mq2", 1024, B)
_buf("mor0 mor1", 4624, B)
_buf("tq0 tq1 tq2", 1024, F)
_buf("tl", 1032, F)
_buf("ydb", 2560, F)
_buf("mvt0 mvt1 dd", 640, B)
_buf("mvp0 mvp1 mpt0 mpt1 eq ee neq", 512, B)
_buf("bst0 bst1 cq", 640, F)
_buf("bsh0 bsh1", 512, H)
_buf("u16", 592, H)
_buf("dro0 dro1 cdo eo", 512, U)
_buf("rep0 rep1 dr es", 4096, B)
_buf("dm gd", 8192, B)
_buf("g2", 2048, B)
_buf("cdf ks", 512, F)
_buf("ec", 512, I)
_buf("us", 256, F)
_buf("junk", 320, B)
_buf("ia ib pi", 32, I)
_buf("ja jb jc", 8, I)
_buf("kap", 192, U)
_buf("kin", 192, I)
_buf("zin", 96, I)
_buf("wo po0 po1 ua ub", 32, U)
_buf("sel blk w2o", 8, U)
_buf("i16 wf fa fb fc ha hb", 32, F)
_buf("old tgt dpos epos", 96, F)
_buf("cumw bc", 40, F)
_buf("fw fs", 40, B)
_buf("tg2 f2 o2", 16, F)
_buf("uc", 16, U)
_buf("gw", 32, B)
_buf("mh dw vw", 32, H)
_buf("col", 8, F)
_buf("acc bj ga sf", 8, F)
_buf("gb", 8, B)
_buf("c2f bs2", 128, F)
_buf("ec2 ea2", 128, I)
_buf("c2o eo2", 128, U)
_buf("mv2 mt2 dd2 ee2 cmp", 128, B)
_buf("rm zsp la1 la2", 1024, B)
_buf("minm vrh vrl0 vrl1", 512, B)
_buf("xp", 2048, B)
_buf("dg", 2080, B)
_buf("m8 m8r", 256, B)
_buf("id1 srow", 128, F)
_buf("b1 tri ust idh idn idb one", 128, B)
_buf("m0p m0n m0w", 144, B)
_buf("g8 g8p g8n", 8, B)
_buf("pK pX0 pX1 pG pS pU pB pF", 512, F, P_)
SEMAPHORES = ["cv", "cs", "cp", "cg"] + ["d%d" % i for i in range(40)] + ["rl%d" % i for i in range(9)] + ["ar%d" % i for i in range(9)]
BIG = float(2 ** 25)
SIZE = {F: 4, I: 4, B: 2, H: 2, U: 2}
SEARCH = ("vvvvvvvvssssssss", "rrrrrrrrssssssss", "rrrrrrrrssssssss")
KEYS = ((0, 2, 1, 3), (2, 3, 0, 1), (2, 3, 0, 1))
ASK = "vsvv"
DWHO = ("ssvsvsvs", "ssssssss", "ssssssss")
EWHO = ("svsvsvss", "svsvsvss", "svsvsvss")
CY, GAT, SCA, HOP = 0.00085, 1.56, 3.8, 0.17
ORDER = []
PASSES = 16


def arrange(ops):
    n = len(ops)
    fwd, bwd = [[] for _ in ops], [[] for _ in ops]
    for j, o in enumerate(ops):
        for i, wait in o["deps"].items():
            gap = ops[i]["lat"] + HOP if wait else 0.0
            fwd[i].append((j, gap))
            bwd[j].append((i, gap))

    def place(nxt, prv, rank, first):
        left = [len(p) for p in prv]
        ready = list(first)
        free, pool = {}, {}
        for i, o in enumerate(ops):
            free[o["q"]] = 0.0
            pool.setdefault(o["q"], [])
            if not left[i]:
                pool[o["q"]].append(i)
        order, end, pick = [], [0.0] * n, {}
        while len(order) < n:
            for q in pool:
                if pool[q] and q not in pick:
                    now = max(free[q], min(ready[i] for i in pool[q]))
                    top = max(pool[q], key=lambda i: (ready[i] <= now, rank[i], -i))
                    c = ops[top]["cost"]
                    soon = [i for i in pool[q] if now < ready[i] <= now + 0.5 * c and rank[i] > rank[top] + c]
                    if soon:
                        top = max(soon, key=lambda i: rank[i])
                        now = ready[top]
                    pick[q] = (now, top)
            now, i = min(pick.values())
            q = ops[i]["q"]
            del pick[q]
            pool[q].remove(i)
            end[i] = free[q] = now + ops[i]["cost"]
            order.append(i)
            for j, gap in nxt[i]:
                ready[j] = max(ready[j], end[i] + gap)
                left[j] -= 1
                if not left[j]:
                    pool[ops[j]["q"]].append(j)
                    pick.pop(ops[j]["q"], None)
        return order, end

    tail = [o["lat"] for o in ops]
    rank = [0.0] * n
    for i in range(n - 1, -1, -1):
        rank[i] = ops[i]["cost"] + max([tail[i]] + [rank[j] + gap for j, gap in fwd[i]])
    best = None
    for p in range(PASSES):
        order, end = place(fwd, bwd, rank, [0.0] * n)
        span = max(e + t for e, t in zip(end, tail))
        if best is None or span < best[0]:
            best = (span, order)
        rank = [r + 0.3 * ((i * 7919 + p * 104729) % 1000) / 1000 for i, r in enumerate(place(bwd, fwd, end, tail)[1])]
    return best[1]


def rank_program(g, core, T, topo):
    rank = T.rank_of(core)
    if rank is None:
        return
    ops, log = [], {}

    def X(name, lo=0, hi=None, st=1):
        name, at, n = PART[name]
        lo, hi = at + lo, at + (n if hi is None else hi)
        return (T[name][:, lo:hi] if st == 1 else T[name][:, lo:hi:st], name, lo, hi, st)

    def X0(name):
        hi = SCRATCH[name][1][1]
        return (T[name][0:1, 0:hi], name, 0, hi, 1)

    def cnt(v):
        return 16 * cnt(v[2]) if len(v) == 3 else len(range(v[2], v[3], v[4]))

    def meet(a, lo, hi, st):
        if a[1] <= lo or hi <= a[0]:
            return False
        return not (st > 1 and a[2] == st and (a[0] - lo) % st)

    def emit(q, fn, R, W, cost, sem=None, n=1, tot=None, lat=0.0, after=()):
        me = len(ops)
        comp = sem is None
        deps = {d: False for d in after}
        touch = [(v[1], v[2], v[3], v[4] if comp else 1, False) for v in R] + [(v[1], v[2], v[3], v[4] if comp else 1, True) for v in W]
        for name, lo, hi, st, w in touch:
            ps = SCRATCH[name][0] == P_
            for rec in log.get(name, []):
                o = ops[rec[4]]
                same = comp and o["comp"] and o["q"] == q
                if ps and same and q == "p":
                    deps.setdefault(rec[4], False)
                elif ps and not same:
                    deps[rec[4]] = True
                elif (w or rec[3]) and meet(rec, lo, hi, st if o["comp"] else 1):
                    deps[rec[4]] = True
        ops.append(dict(q=q, fn=fn, cost=cost, lat=lat, deps=deps, comp=comp, sem=sem, n=n, tot=tot))
        for name, lo, hi, st, w in touch:
            recs = log.setdefault(name, [])
            if SCRATCH[name][0] == P_:
                recs = [r for r in recs if q != "p" and (r[3] or ops[r[4]]["q"] == q)]
            if w and st == 1:
                recs = [r for r in recs if not (lo <= r[0] and r[1] <= hi)]
            recs.append((lo, hi, st, w, me))
            log[name] = recs
        return me

    nsem, lastdma = [0], {}

    def dma(q, out, in_, R=(), W=(), kb=512, sem=None, tot=None):
        if sem is None:
            sem = "d%d" % nsem[0]
            nsem[0] += 1
        lastdma[q] = emit(q, lambda e: e.dma_start(out, in_), R, W, 0.06, sem=sem, n=16, tot=tot or 16, lat=1.0 + kb / 330,
                          after=[lastdma[q]] if q in lastdma else [])

    def ind(win, off):
        return (win[0].indirect(off[0]), win, off)

    def rd(*vs):
        r = []
        for v in vs:
            if isinstance(v, tuple):
                r += [v[1], v[2]] if len(v) == 3 else [v]
        return r

    def val(k):
        return k[0] if isinstance(k, tuple) else k

    def cost(a, *sides, per=None):
        if len(a) == 3:
            return 0.06 + cnt(a) * GAT * CY
        if per is None:
            per = 0.5 if all(SIZE[SCRATCH[v[1]][2]] == 2 for v in (a,) + sides) else 1
        return max(64, cnt(a) * per) * CY

    def tt(out, a, b, op):
        per = 2 if len(a) != 3 and SCRATCH[a[1]][0] == S_ and SCRATCH[b[1]][0] == S_ else 1
        emit("v", lambda e: e.tensor_tensor(out[0], a[0], b[0], op), rd(a, b), [out], cost(a, per=per))

    def ts(out, a, s1, op0, s2=None, op1=None):
        if op1 is None:
            emit("v", lambda e: e.tensor_scalar(out[0], a[0], val(s1), None, op0), rd(a, s1), [out], cost(a, out))
        else:
            emit("v", lambda e: e.tensor_scalar(out[0], a[0], val(s1), val(s2), op0, op1), rd(a, s1, s2), [out], cost(a, out))

    def cp(out, a):
        if len(out) == 3:
            emit("v", lambda e: e.tensor_copy(out[0], a[0]), [a, out[2]], [out[1]], 0.06 + cnt(a) * SCA * CY)
        else:
            emit("v", lambda e: e.tensor_copy(out[0], a[0]), rd(a), [out], cost(a, out))

    def ms(out, v):
        emit("v", lambda e: e.memset(out[0], v), [], [out], cost(out))

    def scan(out, d0, d1, init, op0, op1):
        emit("v", lambda e: e.tensor_tensor_scan(out[0], d0[0], d1[0], init, op0, op1), [d0, d1], [out], cost(d0, d1, out))

    def act(out, a, func, bias=0.0, scale=1.0, accum=None):
        if accum:
            emit("s", lambda e: e.activation(out[0], a[0], func, bias=val(bias), scale=scale, accum_out=accum[0]), rd(a, bias), [out, accum], cost(a, per=1) + 0.02)
        else:
            emit("s", lambda e: e.activation(out[0], a[0], func, bias=val(bias), scale=scale), rd(a, bias), [out], cost(a, per=1))

    turn, kind = {}, [0]

    def inturn():
        me = len(ops) - 1
        key = (ops[me]["q"], kind[0])
        if key in turn:
            ops[me]["deps"].setdefault(turn[key], False)
        turn[key] = me

    def gather(who, out, src):
        if who == "s":
            act(out, src, AF.Copy)
        else:
            cp(out, src)
        inturn()

    def mm(out, l, r, start, stop):
        c = max(min(64, cnt(l)), cnt(r)) * (4 if SCRATCH[l[1]][2] == F else 1) * CY
        emit("p", lambda e: e.matmul(out[0], l[0], r[0], start, stop), [l, r], [out], c)

    def iota(out, pat, base, cm):
        flt = SCRATCH[out[1]][2] != I
        emit("g", lambda e: e.iota(out[0], pat, base, cm, allow_small_or_imprecise_dtypes=True) if flt else e.iota(out[0], pat, base, cm), [], [out],
             0.13 + 2 * cnt(out) * CY)

    def asel(b, pat, op, base, cm, src=None):
        src = src or b
        emit("g", lambda e: e.affine_select(b[0], src[0], pat, op, 0.0, base, cm), [src], [b], 0.17 + 2 * cnt(b) * CY)

    def gcopy(out, src):
        asel(out, [[0, cnt(out)]], OP.is_ge, 1, 0, src)

    def same(b, o, st):
        asel(b, o + [[-16, 8]] + st, OP.is_ge, 0, 1)
        asel(b, o + [[16, 8]] + st, OP.is_ge, 15, -1)

    def wrap(out, src, n, m="m0p", start=True, stop=True):
        for b in range(16):
            mm(out, X(m, 16 - b, 144 - b), X(src, b, n, 16), start and b == 0, stop and b == 15)

    def shift(b, to):
        lo = 16 + 128 * b - (to - b)
        return X("dg", lo, lo + 128)

    cores = T.cores

    def send(src, dst, t, ix):
        to = cores[(rank - 1 - t) % len(cores)]
        e = topo.engines(core, to)[:8]
        m = sum(1 << k for k in e)
        a = topo.addr(to)
        out = T[dst][:, 0:1024]
        me = emit("g", lambda q: q.remote_dma(out, src[0], T.sem["ar%d" % ix], T.sem["rl%d" % ix], a[1], a[0], m), [src, X("basi")], [], 0.3,
                  sem="rl%d" % ix, n=0, tot=len(e), lat=4.0)
        emit("x", None, [], [X(dst)], 0.0, sem="ar%d" % ix, n=0, tot=len(e), after=[me], lat=4.5)

    dma("s", T.meas[:], T.mea[:], W=[X("meas")], kb=256)
    for c in range(4):
        dma("y", T.bw[:, 16 * c:16 * c + 16], T.bas[15::16, 256 * c:256 * c + 256], W=[X("bw", 16 * c, 16 * c + 16)], kb=8)
    dma("y", T.usei[:], T.use[:], W=[X("usei")], kb=768)
    dma("y", T.dt[:, 0:1024], T.der[:], W=[X("dt", 0, 1024)], kb=1280)
    dma("y", T.mor0[:, 0:2048], T.mor[:], W=[X("mor0", 0, 2048)], kb=1792)
    dma("y", T.basi[:], T.bas[:], W=[X("basi")], kb=2304)
    dma("y", T.mor0[:, 2048:4096], T.mor[:], W=[X("mor0", 2048, 4096)], kb=2816)
    dma("y", T.mor1[:, 0:2048], T.mor[:], W=[X("mor1", 0, 2048)], kb=3300)
    for b in range(16):
        dma("y", T.b15[b::16, 0:994], T.bas[15::16, 2 * b:2 * b + 994], W=[X("b15")] if b == 15 else [], sem="d39", tot=256, kb=3800)

    PK, P16, PEN, WZ, NM, TOT, P4 = [X("col", k, k + 1) for k in range(7)]
    for n, v in (("rm", 1), ("zsp", 0), ("g8", 2048), ("id1", 1), ("idb", 2 ** 23), ("idh", 1), ("idn", -1), ("minm", 0), ("m8", 1),
                 ("m8r", 1), ("b1", 1), ("tri", 1), ("ust", 1), ("one", 1), ("m0p", 0), ("m0n", 0)):
        ms(X(n), float(v))
    ms(X("rm", 0, 1024, 16), 0.0)
    ms(X("minm", 0, 512, 16), BIG)
    ms(X("m8r", 0, 256, 8), 0.0)
    ms(X("dg", 0, 16), 0.0)
    ms(X("dg", 2064, 2080), 0.0)
    for n in ("mvt0", "mvt1", "dd", "cq"):
        ms(X(n, 512, 640), 0.0)
    for n in ("bst0", "bst1"):
        ms(X(n, 512, 640), -2048.0)
    for n in ("mor0", "mor1"):
        ms(X(n, 4096, 4624), 16384.0)
    ms(X("tl", 1024, 1032), float(FAR - 2048))
    ms(X("fw", 32, 40), 1.0)
    ms(NM, 0.0)
    iota(X("pi"), [[0, 32]], 0, 1)
    iota(X("fa"), [[256, 4], [2, 8]], 0, 0)
    iota(X("i16"), [[16, 32]], 0, 0)
    same(X("g8"), [], [])
    for n in ("idh", "id1", "idb", "idn"):
        asel(X(n), [[-1, 128]], OP.is_equal, 0, 1)
    for k in range(16):
        cp(X("xp", k, 2048, 16), X("idh"))
    iota(X0("vrh"), [[256, 4], [0, 8], [16, 16]], 0, 0)
    for par in range(2):
        iota(X0("vrl%d" % par), [[0, 4], [2, 8], [0, 16]], par, 0)
    for x in range(8):
        asel(X("la1", 128 * x, 128 * x + 128), [[0, 8], [-1, 2], [-16, 8]], OP.is_equal, -2 * x, 1, X("one"))
        asel(X("la2", 128 * x, 128 * x + 128), [[0, 8], [-1, 16]], OP.is_equal, -16 * x, 1, X("one"))
    same(X("m8"), [[0, 32]], [])
    ts(X("m8"), X("m8"), 4096.0, OP.mult, -4096.0, OP.add)
    for n in ("b1", "tri", "ust"):
        same(X(n), [], [[0, 16]])
    asel(X("tri"), [[1, 128]], OP.is_ge, 0, -1)
    asel(X("ust"), [[-1, 128]], OP.is_gt, 0, 1)
    iota(X("srow"), [[1, 128]], 0, 0)
    ts(X("g8p"), X("g8"), 2.0, OP.mult)
    ts(X("g8n"), X("g8"), -1.0, OP.mult)
    ts(X("m0p", 16, 144, 16), X("g8"), 1 / 2048, OP.mult)
    ts(X("m0n", 16, 144, 16), X("g8"), -1 / 2048, OP.mult)
    ts(X("ia"), X("pi"), 15, OP.bitwise_and)
    cp(PK, X("ia", 0, 1))
    ts(X("fc", 0, 16), X("srow", 0, 16), PK, OP.is_equal)
    for b in range(16):
        ts(X("dg", 16 + 128 * b, 144 + 128 * b), X("idh"), X("fc", b, b + 1), OP.mult)
    ts(P16, PK, 16.0, OP.mult)
    ts(P4, PK, 4.0, OP.mult)
    ts(PEN, PK, 15.0, OP.is_lt, 8192.0, OP.mult)
    ts(WZ, PK, 1.0, OP.add)
    ts(X("m0w"), X("m0p"), WZ, OP.mult)
    ts(X("bj"), X("i16", 0, 8), PK, OP.add, 0.5, OP.add)

    def kap(lo, hi):
        for j in range(lo, hi):
            t = j // 2
            ts(X("kin", 32 * j, 32 * j + 32), X("b15", t % 2, 994, 32) if j % 2 else X("bw", t % 2, 64, 2), 97 * t, OP.add)
        ts(X("kin", 32 * lo, 32 * hi), X("kin", 32 * lo, 32 * hi), 1023, OP.bitwise_and)
        cp(X("kap", 32 * lo, 32 * hi), X("kin", 32 * lo, 32 * hi))

    def flags(par, der, bank):
        mm(X(bank), X("idh"), X("bsh%d" % par), True, True)
        tt(X("neq"), X(bank), der, OP.not_equal)
        mm(X(bank), X("tri"), X("neq"), True, True)
        act(X(bank), X(bank), AF.Relu, bias=PEN, scale=-8192.0)
        tt(X("tl", par, 1024, 2), der, X(bank), OP.subtract)

    def search(t):
        par = t % 2
        kind[0] = "search"
        for h in range(2):
            act(X("cdf", 256 * h, 256 * h + 256), ind(X("usei"), X("kap", 64 * t + 16 * h, 64 * t + 16 * h + 16)), AF.Copy)
            cp(X("cdo", 256 * h, 256 * h + 256), X("cdf", 256 * h, 256 * h + 256))
        mm(X("pB"), X0("one"), X0("vrh"), True, False)
        mm(X("pB"), X0("one"), X0("vrl%d" % par), False, True)
        tt(X("eq"), X("pB"), X("cdf"), OP.is_equal)
        for c in range(16):
            sl = X("dm", 512 * c, 512 * c + 512)
            src = ind(X("meas"), X("cdo", 32 * c, 32 * c + 32))
            how = SEARCH[t][c]
            if how in "vr":
                tt(sl, src, X("rep%d" % par, 512 * c, 512 * c + 512), OP.subtract)
                inturn()
                if how == "v":
                    act(sl, sl, AF.Abs)
                else:
                    ts(X("dr", 512 * c, 512 * c + 512), sl, 0.0, OP.max)
            else:
                bank = X("pF" if c % 2 else "pB" if t else "pU")
                j = c // 4
                gather(how, sl, src)
                mm(bank, X("mpt%d" % par, 128 * j, 128 * j + 128), X("xp", 512 * (c % 4), 512 * (c % 4) + 512), True, False)
                mm(bank, X("idh"), sl, False, True)
                act(sl, bank, AF.Abs)
        for j in KEYS[t]:
            blk = X("pK", 128 * j, 128 * j + 128)
            mm(blk, X("cdf", 128 * j, 128 * j + 128), X("id1"), True, False)
            mm(blk, X("eq", 128 * j, 128 * j + 128), X("idb"), False, False)
            parts = (("dm", "g8n"), ("dr", "g8p")) if SEARCH[t][4 * j] == "r" else (("dm", "g8"),)
            for d, f in parts:
                for k in range(16):
                    mm(X("pK", 128 * j + k, 128 * j + 128, 16), X(d, 2048 * j + k, 2048 * j + 2048, 16), X(f), False, k == 15 and d == parts[-1][0])
        scan(X("ks"), X("minm"), X("pK"), BIG, OP.max, OP.min)
        ts(X("ia"), X("ks", 15, 512, 16), float(2 ** 23 - 1024), OP.min)
        ts(X("ib"), X("ia"), 2047, OP.bitwise_and)
        cp(X("mh"), X("ib"))
        mm(X("pF", 0, 256), X("idh"), X("m8"), True, False)
        for x in range(8):
            mm(X("pF", 32 * x, 32 * x + 32), X("la1", 128 * x, 128 * x + 128), X("mh"), False, x == 7)
        scan(X("us"), X("m8r"), X("pF", 0, 256), 0.0, OP.mult, OP.max)
        for c in range(4):
            cp(X("wo", 8 * c, 8 * c + 8), X("us", 8 * c + 7, 256, 32))
        cp(X("wf"), X("wo"))
        ts(X("ia"), X("wf"), 0.5, OP.mult, -0.25, OP.add)
        ts(X("fa"), X("ia"), 4.0, OP.mult, 1.0, OP.add)
        tt(X("fb"), X("wf"), X("old", 32 * t, 32 * t + 32), OP.add)
        tt(X("dw"), X("fa"), X("fb"), OP.subtract)

    flip = [0]

    def lists(who, win, offs, dist, mv, n, ends):
        lo = 0
        kind[0] = "lists"
        for c, w in enumerate(who):
            k = n // 16
            a = X("gd", n * c, n * c + n)
            gather(w, a, ind(win, X(offs, k * c, k * c + k)))
            e = (n * c) % 4096
            scan(X("es", e, e + n), X("rm", 0, n), a, 0.0, OP.mult, OP.max)
            px = "pX%d" % flip[0]
            mm(X(px, k * c, k * c + k), X("idn"), X(mv, k * c, k * c + k), True, False)
            mm(X(px, k * c, k * c + k), X("idh"), X("es", e + 15, e + n, 16), False, True)
            if c in ends:
                act(X(dist, lo, k * c + k), X(px, lo, k * c + k), AF.Abs)
                lo = k * c + k
                flip[0] ^= 1

    def meanings(par, bank):
        mvp = "mvp%d" % par
        act(X(mvp), ind(X("meas"), X("po%d" % par)), AF.Copy)
        for j in range(2):
            mm(X(bank, 128 * j, 128 * j + 128), X(mvp, 256 + 128 * j, 384 + 128 * j), X("idn"), True, True)
        act(X("mpt%d" % par, 256, 512), X(bank, 0, 256), AF.Copy)
        for c in range(2 * (1 - par)):
            cp(X("zsp", 0, 1024, 16), X(mvp, 64 * c, 64 * c + 64))
            scan(X("rep0", 1024 * c, 1024 * c + 1024), X("rm"), X("zsp"), 0.0, OP.mult, OP.add)
        lo = 2048 * (1 - par)
        for k in range(16):
            gcopy(X("rep%d" % par, lo + k, 4096, 16), X(mvp, lo // 16, 256))

    def targets(par):
        wrap(X("pS", 96, 128), "mvt%d" % par, 512, "m0w")
        for t in range(par, 3, 2):
            w = (32 * t, 32 * t + 32)
            ts(X("zin", *w), X("pS", 96, 128), float(t), OP.add)
            ts(X("zin", *w), X("zin", *w), 3, OP.bitwise_and)
            tt(X("tgt", *w), X("tgt", *w), X("zin", *w), OP.add)

    send(X("meas"), "mq0", 0, 0)
    kap(0, 1)
    for par in range(2):
        ts(X("po%d" % par), X("fa"), P16, OP.add, float(par), OP.add)
    meanings(0, "pX0")
    for par in range(2):
        gcopy(X("mvt%d" % par, 0, 512), X("meas", par, 1024, 2))
        (gcopy if par else cp)(X("dro%d" % par), X("dt", par, 1024, 2))
        gcopy(X("bsh%d" % par), X("basi", par, 1024, 2))
        ts(X("bst%d" % par, 0, 512), X("basi", par, 1024, 2), -2048.0, OP.add)
    send(X("usei"), "uq0", 0, 1)
    gcopy(X("u16"), X("usei", 0, 592))
    for t in range(3):
        for b in range(16):
            mm(X("pS", 32 * t, 32 * t + 32), shift((b + t) % 16, b), X("u16", 37 * t + b, 37 * t + 512, 16), b == 0, b == 15)
    cp(X("old"), X("pS", 0, 96))
    search(0)
    meanings(1, "pU")
    for par in range(2):
        flags(par, X("dt", par, 1024, 2), ("pB", "pG")[par])
    send(X("tl", 0, 1024), "tq0", 0, 2)
    kap(1, 6)
    iota(X("tgt"), [[0, 3], [64, 32]], 0, 0)
    ts(X("tgt"), X("tgt"), P4, OP.add)
    targets(0)
    iota(X("epos", 0, 64), [[0, 2], [16, 32]], E0, 0)
    iota(X("epos", 64, 96), [[16, 32]], 0, 0)
    ts(X("epos"), X("epos"), PK, OP.add)
    iota(X("dpos", 0, 64), [[1, 2], [16, 32]], -E0, 0)
    ts(X("dpos", 0, 64), X("dpos", 0, 64), PK, OP.add)
    ms(X("dpos", 64, 96), 512.0)
    send(X("meas"), "mq1", 1, 3)
    send(X("meas"), "mq2", 2, 6)

    for t in range(3):
        par = t % 2
        mvt, bst, mor, nxt = "mvt%d" % par, "bst%d" % par, "mor%d" % par, "mor%d" % (1 - par)
        w = (32 * t, 32 * t + 32)
        if t:
            dma("y", T[mor][:, 2048:4096], T[mor][:, 0:2048], R=[X(mor, 0, 2048)], W=[X(mor, 2048, 4096)])
            dma("y", T[nxt][:, 0:2048], T[mor][:, 0:2048], R=[X(mor, 0, 2048)], W=[X(nxt, 0, 2048)], kb=1024)
        lists(DWHO[t], X(mor, 0, 2048), "dro%d" % par, "dd", mvt, 1024, (3, 7))
        wrap(X("pG", 0, 32), "dd", 512, "m0n", True, False)
        for h in range(2):
            l = (256 * h, 256 * h + 256)
            tt(X("ec", *l), ind(X("tl"), X("wo", 16 * h, 16 * h + 16)), X(bst, *l), OP.max)
            ts(X("eo", *l), X("ec", *l), 2048.0, OP.add)
        ts(X("dt", E0, E0 + 512), X("ec"), 2047, OP.bitwise_and)
        lists(EWHO[t], X(mor), "eo", "ee", mvt, 1024, (3, 6, 7))
        wrap(X("pG", 0, 32), "ee", 512, "m0p", False, True)
        ts(X("fw", 0, 32), X("pG", 0, 32), NM, OP.is_ge)
        ts(X("gw"), X("pG", 0, 32), NM, OP.is_lt)
        mm(X("pS", 0, 40), X("b1"), X("fw"), True, True)
        mm(X("pS", 256, 296), X("ust"), X("fw"), True, True)
        scan(X("bc"), X("one", 0, 40), X("pS", 0, 40), 0.0, OP.mult, OP.add)
        tt(X("cumw"), X("bc"), X("pS", 256, 296), OP.subtract)
        for a in range(8):
            act(X("junk", 40 * a, 40 * a + 40), X("bc"), AF.Sign, bias=X("bj", a, a + 1), scale=-1.0, accum=X("acc", a, a + 1))
        ts(X("blk"), X("acc"), 0.5, OP.mult, 20.0, OP.add)
        tt(X("cmp"), ind(X("cumw"), X("blk")), X("srow"), OP.is_le)
        act(X("gb"), X("acc"), AF.Copy, bias=320.0, scale=8.0)
        mm(X("pS", 64, 72), X("idh"), X("gb"), True, False)
        wrap(X("pS", 64, 72), "cmp", 128, start=False)
        cp(X("sel"), X("pS", 64, 72))
        cp(X("sf"), X("pS", 64, 72))
        tt(X("vw"), X("dw"), X("gw"), OP.mult)
        for b in range(16):
            mm(X("pB", b, 512, 16), shift(b, (b + t) % 16), X("vw"), True, True)
        us = X("usei", 37 * t, 37 * t + 512)
        act(X("cq", 0, 512), ind(X("uq%d" % t), X("kap", 64 * t + 32, 64 * t + 64)), AF.Copy)
        tt(us, X("pB"), us, OP.add)
        if t < 2:
            send(X("usei"), "uq%d" % (t + 1), t + 1, 4 if t == 0 else 7)
        else:
            gcopy(X("tq0"), X("usei"))
            dma("y", T.yu[:], T.tq0[:], R=[X("tq0")])
        new = X("dt", D0, D0 + 512) if t == 0 else X("ydb", par, 1024, 2)
        tt(X("ha"), X("fw", 0, 32), X("dpos", *w), OP.mult)
        tt(X("hb"), X("ha"), X("epos", *w), OP.add)
        cp(X("ua"), X("hb"))
        cp(new, ind(X("dt", 0, D0) if t < 2 else X("dt", E0, D0 + 512), X("ua")))
        ts(X("fs", 0, 32), X("fw", 0, 32), float(SH), OP.mult)
        tt(X("fc"), X("fs", 0, 32), X("tgt", *w), OP.add)
        cp(X("ub"), X("fc"))
        for h in range(4):
            cp(ind(X(nxt, 0, FAR), X("ub", 8 * h, 8 * h + 8)), X(mvt, 128 * h, 128 * h + 128))
        cp(X("c2o"), ind(X("cq"), X("sel")))
        act(X("mv2"), ind(X(mvt), X("sel")), AF.Copy)
        act(X("c2f"), ind(X("cq"), X("sel")), AF.Copy)
        mm(X("pS", 128, 256), X("mv2"), X("idn"), True, True)
        act(X("mt2"), X("pS", 128, 256), AF.Copy)
        mm(X("pU", 0, 128), X("c2f"), X("id1"), True, False)
        kind[0] = "lists"
        for q in range(4):
            a = X("g2", 512 * q, 512 * q + 512)
            px = X("pX%d" % (q % 2))
            src = ind(X("mq%d" % t), X("c2o", 32 * q, 32 * q + 32))
            if ASK[q] == "v":
                rp = X("es", 2048 + 512 * q, 2560 + 512 * q)
                z = 512 * (q % 2)
                cp(X("zsp", z, z + 512, 16), X("mv2", 32 * q, 32 * q + 32))
                scan(rp, X("rm", 0, 512), X("zsp", z, z + 512), 0.0, OP.mult, OP.add)
                tt(a, src, rp, OP.subtract)
                inturn()
                act(a, a, AF.Abs)
            else:
                gather(ASK[q], a, src)
                mm(px, X("mt2"), X("xp", 512 * q, 512 * q + 512), True, False)
                mm(px, X("idh"), a, False, True)
                act(a, px, AF.Abs)
            for k in range(16):
                o = X("pU", k, 128, 16)
                mm((T.pU[32 * q:32 * q + 32, k:128:16],) + o[1:], X("g2", 512 * q + k, 512 * q + 512, 16), X("g8"), False, k == 15)
        act(X("dd2"), ind(X("dd"), X("sel")), AF.Copy)
        act(X("bs2"), ind(X(bst), X("sel")), AF.Copy)
        wrap(X("pG", 32, 40), "dd2", 128, "m0n", True, False)
        wrap(X("pS", 72, 80), "mv2", 128, "m0w")
        ts(X("ja"), X("pS", 72, 80), float(t), OP.add)
        ts(X("jb"), X("ja"), 3, OP.bitwise_and)
        act(X("ga"), X("sf"), AF.Copy, scale=4.0)
        tt(X("tg2", 0, 8), X("ga"), X("jb"), OP.add)
        act(X("tg2", 8, 16), X("sf"), AF.Copy, scale=2.0 if t else 1.0, bias=float(par))
        scan(X("ks", 0, 128), X("minm", 0, 128), X("pU", 0, 128), BIG, OP.max, OP.min)
        cp(X("ja"), X("ks", 15, 128, 16))
        ts(X("jc"), X("ja"), 2047, OP.bitwise_and)
        cp(X("mh", 0, 8), X("jc"))
        mm(X("pU", 256, 320), X("idh"), X("m8", 0, 64), True, False)
        for x in range(8):
            mm(X("pU", 256 + 8 * x, 264 + 8 * x), X("la2", 128 * x, 128 * x + 128), X("mh", 0, 8), False, x == 7)
        scan(X("us", 0, 64), X("m8r", 0, 64), X("pU", 256, 320), 0.0, OP.mult, OP.max)
        cp(X("w2o"), X("us", 7, 64, 8))
        tt(X("ec2"), ind(X("tq%d" % t), X("w2o")), X("bs2"), OP.max)
        ts(X("eo2"), X("ec2"), 2048.0, OP.add)
        ts(X("ea2"), X("ec2"), 2047, OP.bitwise_and)
        lists("svsv", X(mor), "eo2", "ee2", "mv2", 512, (3,))
        wrap(X("pG", 32, 40), "ee2", 128, "m0p", False, True)
        ts(X("f2", 0, 8), X("pG", 32, 40), NM, OP.is_ge, float(SH), OP.mult)
        ts(X("f2", 8, 16), X("pG", 32, 40), NM, OP.is_ge, 1280.0 if t else 640.0, OP.mult)
        tt(X("o2"), X("f2"), X("tg2"), OP.add)
        cp(X("uc"), X("o2"))
        cp(ind(X(nxt, 0, FAR), X("uc", 0, 8)), X("mv2"))
        cp(ind(X("ydb") if t else X("dt", D0, 2816), X("uc", 8, 16)), X("ea2"))
        if t < 2:
            search(t + 1)
            flags(par, new, "pB")
            send(X("tl", 0, 1024), "tq%d" % (t + 1), t + 1, 5 if t == 0 else 8)
            act(X("fs", 32, 40), X("f2", 0, 8), AF.Copy)
            mm(X("pS", 80, 120), X("one"), X("fs"), True, True)
            act(X("bc"), X("pS", 80, 120), AF.Copy, accum=TOT)
            ts(X("ja", 0, 1), TOT, -1.0 / SH, OP.mult)
            ts(X("jb", 0, 1), X("ja", 0, 1), 127, OP.bitwise_and)
            ts(NM, X("jb", 0, 1), -1.0, OP.mult)
        if t == 0:
            gcopy(X("dro0"), new)
            targets(1)
    dma("s", T.ym[:], T.mor1[:, 0:2048], R=[X("mor1", 0, 2048)])
    dma("y", T.yd[:], T.ydb[:, 0:1024], R=[X("ydb", 0, 1024)])

    if not ORDER:
        ORDER.extend(arrange(ops))
    queue = {"v": g.vector, "s": g.scalar, "p": g.tensor, "g": g, "y": g.sync}
    clock = {q: {} for q in queue}
    total = {}
    for pos, i in enumerate(ORDER):
        o = ops[i]
        q = o["q"]
        o["pos"] = pos
        if q == "x":
            total[o["sem"]] = o["tot"]
            o["at"], o["known"] = (o["sem"], o["tot"]), {o["sem"]: o["tot"]}
            continue
        for d in sorted((d for d, wait in o["deps"].items() if wait), key=lambda d: -ops[d]["pos"]):
            s, c = ops[d]["at"]
            if clock[q].get(s, 0) < c:
                queue[q].wait_ge(T.sem[s], c)
                for s2, c2 in ops[d]["known"].items():
                    clock[q][s2] = max(clock[q].get(s2, 0), c2)
        s = "c" + q if o["comp"] else o["sem"]
        ins = o["fn"](queue[q])
        if o["n"]:
            ins.then_inc(T.sem[s], o["n"])
        total[s] = total.get(s, 0) + 1 if o["comp"] else o["tot"]
        o["at"] = (s, total[s])
        o["known"] = dict(clock[q])
        o["known"][s] = total[s]
    for s in sorted(total):
        if clock["g"].get(s, 0) < total[s]:
            g.wait_ge(T.sem[s], total[s])
